import numpy as np, ml_dtypes
CORES = [1,5,17,21,33,37,49,53]
N = 8
BF = ml_dtypes.bfloat16
def gentries(a):
    return np.ascontiguousarray(a.reshape(8, 16, -1).transpose(0, 2, 1)).reshape(8, -1)
def gtable(e):
    e = np.asarray(e); return np.ascontiguousarray(e.reshape(8, -1, 16).transpose(0, 2, 1)).reshape(128, -1).astype(np.int32)
W, LW, C, B, KEYS, Q, RO = 2048, 11, 256, 8, 8, 7, 3
def pick(T, c):
    L = np.ascontiguousarray(c.transpose(0, 1, 3, 2)).reshape(N * 8, 16 * C)
    return np.stack([np.take(a, l, axis=1) for a, l in zip(T.reshape(N * 8, 16, W), L)]).reshape(N, 8, 16, C, 16)
def ask(D, X, c, y, w):
    d = pick(D, c); same = (d & (KEYS - 1)) == (c & (KEYS - 1))[..., None]
    cp = np.maximum(c, np.max(np.where(same, d, 0), axis=4))
    x = pick(X, cp); z = (np.max(x, axis=4) + np.min(x, axis=4)) >> 1
    u = np.add.reduce(w * z, axis=2, keepdims=True) & 4095
    return cp, z, u, B * np.arange(C) + (u & (B - 1)), np.abs(z - y)
def put(T, pl, val):
    np.put_along_axis(T, pl, val, axis=3)
def far(X, cp, v):
    return np.add.reduce(np.abs(pick(X, cp) - v[..., None]), axis=2)
def eve(D, X, c, y, w):
    cp, z, u, pl, v = ask(D, X, c, y, w); X = X.copy(); put(X, pl, v)
    return np.sort(far(X, np.roll(cp, 1, axis=0), np.roll(v, 1, axis=0)), axis=-1)[..., Q - 1]
def level(rng, q):
    return np.take_along_axis(np.sort(q, axis=-1), rng.integers(C // 4, 3 * C // 4, (N, 8, 1)), 2)[..., 0]
def sums(rng, tot):
    a = (tot[:, None, :] + np.arange(16).reshape(16, 1)) >> 4; hi, lo = a[:, :8], a[:, 8:]
    e = np.floor(rng.random((N, 8, C)) * (np.minimum(255 - hi, lo) + 1)).astype(np.int64)
    return rng.permuted(np.concatenate([hi + e, lo - e], axis=1), axis=1)
def parts(rng):
    D = rng.integers(0, W, (N, 8, 16, W)); X = (rng.random((N, 8, 16, W)) * rng.integers(64, 257, (N, 8, 1, W))).astype(np.int64)
    c = rng.integers(0, W, (N, 8, 16, C)); y = rng.integers(0, 256, (N, 8, 16, C)); w = rng.integers(0, 16, (N, 8, 16, C)); m = rng.integers(0, 2048, (N, 8, 16, 1))
    return D, X, c, y, w, m
def pack(D, X, c, y, w, m, th):
    return {"rec": (W * X + D).reshape(N, 128, W).astype(np.int32), "req": np.stack([gtable(a.transpose(0, 2, 1).reshape(8, 16 * C)) for a in c]),
            "aim": y.reshape(N, 128, C).astype(np.float32).astype(BF), "wt": w.reshape(N, 128, C).astype(np.float32).astype(BF),
            "mul": m.reshape(N, 128, 1).astype(np.int32), "th": np.repeat(th, 16, axis=1).reshape(N, 128, 1).astype(np.int32)}
def setup_inputs(rng):
    D, X, c, y, w, m = parts(rng)
    return pack(D, X, c, y, w, m, level(rng, eve(D, X, c, y, w)))
def setup_inputs_ties(rng):
    D, X, c, y, w, m = parts(rng); h = C // 2
    put(D, c[..., h:], (c[..., h:] + KEYS) & (W - 1)); put(D, c[..., :h], c[..., :h])
    z = ask(D, X, c, y, w)[1]
    y = np.where(rng.random((N, 8, 1, C)) < 0.3, np.minimum(np.maximum(z + rng.integers(-1, 2, z.shape), 0), 255), y)
    th = level(rng, eve(D, X, c, y, w)) + ((np.arange(8) + np.arange(N)[:, None]) & 1)
    return pack(D, X, c, y, w, m, th)
def setup_inputs_alike(rng):
    D, X, c, y, w, m = parts(rng)
    D[:, 1::2] += KEYS // 2 - (D[:, 1::2] & (KEYS - 1)); c[:, 1::2] += KEYS // 2 - (c[:, 1::2] & (KEYS - 1))
    c[:, 0] = rng.choice(np.array([0, W - 1, W // 2, 5]), (N, 16, C)); c[:, 4] = rng.choice(np.array([0, W - 1, W - 2, KEYS - 1, 7 * KEYS - 1]), (N, 16, C)); c[:, 6] = c[:, 6, :1]
    D[:, 2] = np.arange(W); D[:, 4] = W - 1; D[:, 6] = 0
    X[:, 4] = 255 * rng.integers(0, 2, (N, 1, W))
    return pack(D, X, c, y, w, m, level(rng, eve(D, X, c, y, w)))
def setup_inputs_ends(rng):
    D, X, c, y, w, m = parts(rng)
    th = rng.choice(np.array([0, 1, 4080, 4081]), (N, 8)); q = rng.permutation(N); th[q[0]] = 4081; th[q[1]] = 0
    w[:, 1] = 0
    X[:, 3, :2] = 255; X[:, 3, 2] = 15; w[:, 3] = 0; w[:, 3, 0] = 15; w[:, 3, 1:3] = 1; m[:, 3] = 2047
    y[:, 5] = 255 * rng.integers(0, 2, (N, 16, C)); w[:, 5] = 15; m[:, 5] = 0
    X[:, 7] = 255; y[:, 7] = 255; th[:, 7] = 4080 + (np.arange(N) & 1)
    return pack(D, X, c, y, w, m, th)
def setup_inputs_own(rng):
    D, X, c, y, w, m = parts(rng); lim = 4 * int(rng.integers(513, 1000)) + int(rng.integers(0, 2))
    X[:, :2, :, 1::2] = 255; c[:, :2] |= 1; w[:, :2] = w[:, :2, :1]
    y[:, 0] = sums(rng, rng.choice(np.array([0, 0, 1, 16]), (N, C))); y[:, 1] = sums(rng, lim + rng.integers(-2, 2, (N, C)))
    X[:, 2] = 255 - rng.integers(0, 17, (N, 16, W)); w[:, 2] = 14 + rng.integers(0, 2, (N, 16, C)); y[:, 2] = y[:, 2] * rng.integers(0, 2, (N, 1, C))
    for g, h in ((3, 127), (4, C - 1), (5, int(rng.choice(np.array([32, 63, 64, C // 2, C - 2]))))):
        D[:, g] = B * h; w[:, g] = 0; c[:, g] = KEYS * rng.integers(0, B * h // KEYS + 1, (N, 16, C))
        b = np.tile(rng.integers(0, 2, (1, 16)), (N, 1)); b[np.arange(N), rng.permutation(16)[:N]] ^= 1
        X[:, g, :, B * h] = KEYS * b; y[:, g] = KEYS * rng.integers(0, 2, (N, 16, C)); y[:, g, :, h] = KEYS
    c[:, 6, :, ::2] = 0; D[:, 6, :, 0] = 0; X[:, 6, :, 0] = 0; y[:, 6, :, 0] = 0
    D[:, 7] = np.arange(W); c[:, 7] = (B * (np.arange(C) + rng.integers(-1, 2, (N, 16, C))) + rng.integers(0, B, (N, 16, C))) & (W - 1)
    th = level(rng, eve(D, X, c, y, w))
    th[:, 0] = (np.arange(N) + int(rng.integers(0, 2))) & 1; th[:, 1] = lim; th[:, 3:6] = 8 * KEYS; th[:, 6] = rng.integers(1900, 2200, N)
    return pack(D, X, c, y, w, m, th)
def setup_inputs_spread(rng):
    D, X, c, y, w, m = parts(rng)
    def uneven(*shape):
        a = np.exp2(LW * rng.random(shape)).astype(np.int64) - 1
        return np.where(rng.random(shape[:-2] + (1, shape[-1])) < 0.5, a, W - 1 - a)
    D = np.where(rng.random((N, 8, 1, W)) < 0.5, uneven(N, 8, 16, W), D); c = np.where(rng.random((N, 8, 1, C)) < 0.5, uneven(N, 8, 16, C), c)
    X = (np.exp2(8 * rng.random((N, 8, 1, W))) * rng.random((N, 8, 16, W))).astype(np.int64)
    y = (np.exp2(8 * rng.random((N, 8, 1, C))) * rng.random((N, 8, 16, C))).astype(np.int64); w = w * (rng.random(w.shape) < rng.random((N, 8, 1, C)))
    m = (np.exp2(11 * rng.random(m.shape))).astype(np.int64)
    return pack(D, X, c, y, w, np.minimum(m, 2047), level(rng, eve(D, X, c, y, w)))
def check_inputs(d):
    bad = []
    for k, lo, hi in (("rec", 0, 256 * W - 1), ("req", 0, W - 1), ("aim", 0, 255), ("wt", 0, 15), ("mul", 0, 2047), ("th", 0, 4081)):
        a = np.asarray(d[k]).astype(np.float64)
        if not (np.min(a) >= lo and np.max(a) <= hi): bad.append("range of " + k)
        if not np.all(a == np.floor(a)): bad.append("whole numbers in " + k)
    a = np.asarray(d["th"]).reshape(N, 8, 16)
    if np.any(a != a[:, :, :1]): bad.append("th alike in the rows of a group")
    return bad
def reference(rec, req, aim, wt, mul, th):
    R = rec.astype(np.int64).reshape(N, 8, 16, W); D = R & (W - 1); X = R >> LW
    c = req.astype(np.int64).reshape(N, 8, 16, C)
    y = aim.astype(np.int64).reshape(N, 8, 16, C); w = wt.astype(np.int64).reshape(N, 8, 16, C)
    m = mul.astype(np.int64).reshape(N, 8, 16, 1); lim = th.astype(np.int64).reshape(N, 8, 16)[:, :, 0]
    odd = 2 * np.arange(16).reshape(16, 1) + 1
    for t in range(RO):
        cp, z, u, pl, v = ask(D, X, c, y, w)
        put(D, pl, cp); put(X, pl, v)
        sh = 1 + t % (N - 1)
        ca = np.roll(cp, sh, axis=0); va = np.roll(v, sh, axis=0); pa = np.roll(pl, sh, axis=0)
        near = np.add.reduce((far(X, ca, va) < lim[:, :, None, None]).astype(np.int64), axis=3)
        ok = (near >= Q)[:, :, None, :]
        put(D, pa, np.where(ok, ca, np.take_along_axis(D, pa, 3))); put(X, pa, np.where(ok, va, np.take_along_axis(X, pa, 3)))
        c = (((u * u) >> 5) + m * u + odd * z) & (W - 1)
    return {"yc": c.reshape(N, 128, C).astype(np.float32), "yz": z.reshape(N, 128, C).astype(np.float32).astype(BF), "yx": X.reshape(N, 128, W).astype(np.float32).astype(BF)}

@@ -1,0 +1,418 @@
+from concourse.mybir import AluOpType, ActivationFunctionType
+
+A = AluOpType
+F = ActivationFunctionType
+STEPS = 3
+CHUNKS = [(0, 64), (64, 128), (128, 192), (192, 256)]
+PARTS = [(0, 192), (192, 256)]
+NAMES = "AVAV"
+JUDGE = "AAVV"
+SCHED = ("X n1 U1 U0 A0 A2 b1 r0 n3 s0 r1 g0 r2 s1 g1 b3 s2 h0 h1 g2 r3 i0 s3 i1 h2 g3 i2 p0 h3 i3 q0 p1 x0 q1 T0 x1 "
+         "J0 j2 k2 Z N e2 d1 P j3 J1 e0 d0 k3 e1 L v0 D0 e3 v1 D1 K1 K3")
+SCHEDL = ("X n1 U1 U0 A0 A2 b1 r0 n3 s0 r1 g0 r2 s1 g1 b3 s2 h0 h1 g2 r3 i0 s3 i1 h2 g3 i2 p0 h3 i3 q0 p1 x0 q1 T0 x1 "
+          "J0 j2 k2 Z N e2 P j3 J1 e0 Y k3 e1 v0 e3 E0 v1 E1")
+BIG = 16384.0
+ROUND = 12582912.0
+WID = 16 * max(hi - lo for lo, hi in CHUNKS)
+
+SCRATCH = {"psS": ("psum", [128, 1024], "float32"), "psV": ("psum", [128, 512], "float32"), "psE": ("psum", [128, 512], "float32"),
+           "psU": ("psum", [128, 512], "float32"), "psP": ("psum", [128, 512], "float32"), "psN": ("psum", [128, 512], "float32"),
+           "psT": ("psum", [128, 1024], "bfloat16"), "ab": ("sbuf", [128, 16, 16, 16], "bfloat16")}
+for _d, _w, _names in (
+        ("int32", 4096, "dw"), ("bfloat16", 4096, "xw yo"), ("int32", 2048, "reci ra rb"), ("float32", 2048, "xt"),
+        ("int32", 1, "muli thi"), ("float32", 1, "kcol tcol ocol"), ("int32", 128, "p8 pa pb pc"), ("uint16", 128, "pm"),
+        ("int32", 256, "reqi ni ki ui u7 uu sq sh s1 s2 cr"), ("bfloat16", 256, "aimb wtb k5 kt vt zb u7b u7c okm cnt"),
+        ("float32", 256, "pf pfm mm zw yco"), ("uint16", 256, "cl"), ("float32", 128, "bo32"),
+        ("bfloat16", 128, "bt bo idb nidb hid mhalf odd"), ("float16", 128, "idh"), ("bfloat16", 1024, "ones"),
+        ("bfloat16", 2048, "en sel"), ("bfloat16", WID, "nb rm"), ("bfloat16", 16, "ic ic8"), ("float32", 16, "t1 t2"),
+        ("uint16", 16, "plu off"), ("bfloat16", 4096, "kz kb vz vb xb yb sc xg mx mn dg gx"), ("float16", 4096, "xh")):
+    for _n in _names.split():
+        SCRATCH[_n] = ("sbuf", [128, _w], _d)
+for _t in range(STEPS):
+    for _n, _w, _d in (("cp", 256, "uint16"), ("vv", 256, "bfloat16"), ("pl", 16, "float32")):
+        SCRATCH["%s%d" % (_n, _t)] = SCRATCH["a%s%d" % (_n.replace("vv", "v"), _t)] = ("sbuf", [128, _w], _d)
+SEMAPHORES = ["sv", "sa", "sp", "sg", "ls", "l_req", "l_aim", "l_wt", "l_mul", "l_th", "l_rec0", "l_rec1", "o_yc", "o_yz", "o_yx0", "o_yx1"]
+for _t in range(STEPS):
+    SEMAPHORES += ["rp%d" % _t] + ["r%s%d_%d" % (_x, _t, _c) for _x in "cv" for _c in range(len(CHUNKS))]
+
+
+def tracker(g, T):
+    Q = {"v": g.vector, "a": g.scalar, "p": g.tensor, "g": g, "s": g.sync}
+    SEM = {"v": "sv", "a": "sa", "p": "sp", "g": "sg"}
+    count, hist, snap = {}, {}, {}
+    known = {q: {} for q in Q}
+
+    def need(q, outs, ins):
+        req = {}
+        for lst, isw in ((ins, False), (outs, True)):
+            for (_, name, lo, hi) in lst:
+                ps = name[:2] == "ps"
+                for (l2, h2, q2, src, n, w2) in hist.get(name, ()):
+                    over = lo < h2 and l2 < hi
+                    if q2 == q:
+                        hit = over and w2
+                    elif ps:
+                        hit = lo // 512 <= (h2 - 1) // 512 and l2 // 512 <= (hi - 1) // 512
+                    else:
+                        hit = over and (isw or w2)
+                    if hit:
+                        req[src] = max(req.get(src, 0), n)
+        k = known[q]
+        for src in sorted(req, key=lambda s: -req[s]):
+            n = req[src]
+            if k.get(src, 0) >= n:
+                continue
+            Q[q].wait_ge(T.sem[src], n)
+            k[src] = n
+            for s2, n2 in snap.get((src, n), {}).items():
+                if k.get(s2, 0) < n2:
+                    k[s2] = n2
+
+    def note(q, src, n, outs, ins, kq=None):
+        snap[(src, n)] = dict(known.get(kq or q, {}))
+        for lst, isw in ((ins, False), (outs, True)):
+            for (_, name, lo, hi) in lst:
+                h = hist.setdefault(name, [])
+                if isw and name[:2] != "ps":
+                    h[:] = [e for e in h if not (lo <= e[0] and e[1] <= hi)]
+                else:
+                    h[:] = [e for e in h if not (e[0] == lo and e[1] == hi and e[2] == q and e[5] == isw)]
+                h.append((lo, hi, q, src, n, isw))
+
+    def op(q, calls, outs, ins):
+        need(q, outs, ins)
+        for c in calls:
+            i = c()
+        s = SEM[q]
+        i.then_inc(T.sem[s], 1)
+        count[s] = count.get(s, 0) + 1
+        note(q, s, count[s], outs, ins)
+
+    def dma(q, sem, out, in_):
+        o, i = [out] if out[1] else [], [in_] if in_[1] else []
+        need(q, o, i)
+        Q[q].dma_start(out[0], in_[0]).then_inc(T.sem[sem], 16)
+        count[sem] = 16
+        note("dma", sem, 16, o, i, q)
+
+    return op, dma, need, note, count
+
+
+def rank_program(g, core, T, topo):
+    rank = T.rank_of(core)
+    if rank is None:
+        return
+    op, dma, need, note, count = tracker(g, T)
+    V, S, P = g.vector, g.scalar, g.tensor
+    N = len(T.cores)
+    nc = len(CHUNKS)
+
+    def b(name, lo=0, hi=None, st=1):
+        w = T[name].shape[1]
+        hi = w if hi is None else hi
+        if lo == 0 and hi == w and st == 1:
+            return (T[name][:], name, lo, hi)
+        return (T[name][:, lo:hi:st] if st > 1 else T[name][:, lo:hi], name, lo, hi)
+
+    def hbm(t): return (t[:], None, 0, 0)
+    def ind(win, off): return T[win[1]][:, win[2]:win[3]].indirect(off[0])
+    def copy(o, i): op("v", [lambda: V.tensor_copy(o[0], i[0])], [o], [i])
+    def tt(o, x, y, f): op("v", [lambda: V.tensor_tensor(o[0], x[0], y[0], f)], [o], [x, y])
+
+    def tsc(o, x, a, f, a2=None, f2=None):
+        ins = [x] + ([a] if isinstance(a, tuple) else [])
+        va = a[0] if isinstance(a, tuple) else a
+        if f2 is None:
+            op("v", [lambda: V.tensor_scalar(o[0], x[0], va, None, f)], [o], ins)
+        else:
+            op("v", [lambda: V.tensor_scalar(o[0], x[0], va, a2, f, f2)], [o], ins)
+
+    def fill(o, c): op("v", [lambda: V.memset(o[0], c)], [o], [])
+    def scan(o, d0, d1, f0, f1): op("v", [lambda: V.tensor_tensor_scan(o[0], d0[0], d1[0], 0.0, f0, f1)], [o], [d0, d1])
+
+    def act(o, i, f, bias=0.0, scale=1.0):
+        col = [scale] if isinstance(scale, tuple) else []
+        sc = scale[0] if col else scale
+        op("a", [lambda: S.activation(o[0], i[0], f, bias=bias, scale=sc)], [o], [i] + col)
+
+    def gact(o, win, off, f, bias=0.0, scale=1.0):
+        op("a", [lambda: S.activation(o[0], ind(win, off), f, bias=bias, scale=scale)], [o], [win, off])
+
+    def gtt(o, win, off, y, f): op("v", [lambda: V.tensor_tensor(o[0], ind(win, off), y[0], f)], [o], [win, off, y])
+    def put(win, off, val): op("v", [lambda: V.tensor_copy(ind(win, off), val[0])], [win], [off, val])
+    def affine(o, i, pat, f, base, cm): op("g", [lambda: g.affine_select(o[0], i[0], pat, f, 0.0, base, cm)], [o], [i])
+    def iota(o, pat, cm): op("g", [lambda: g.iota(o[0], pat, 0, cm)], [o], [])
+
+    def mms(o, terms):
+        k = len(terms) - 1
+        op("p", [lambda j=j, l=l, r=r: P.matmul(o[0], l[0], r[0], j == 0, j == k) for j, (l, r) in enumerate(terms)],
+           [o], [x for t in terms for x in t])
+
+    def sel(r): return b("sel", 128 * r, 128 * r + 128)
+
+    def eng(src, dst): return topo.engines(src, dst)[:8]
+    for t in range(STEPS):
+        n = len(eng(T.cores[(rank - 1 - t) % N], core))
+        for c, (lo, hi) in enumerate(CHUNKS):
+            for x, nm in (("c", "acp%d"), ("v", "av%d")):
+                note("r", "r%s%d_%d" % (x, t, c), n, [b(nm % t, lo, hi)], [])
+                count["r%s%d_%d" % (x, t, c)] = n
+        note("r", "rp%d" % t, n, [b("apl%d" % t)], [])
+        count["rp%d" % t] = n
+    count["ls"] = 0
+
+    def send(t, dname, sname, sem, lo, hi):
+        dst = T.cores[(rank + 1 + t) % N]
+        es = eng(core, dst)
+        need("g", [], [b(sname, lo, hi)])
+        ad = topo.addr(dst)
+        g.remote_dma(b(dname, lo, hi)[0], b(sname, lo, hi)[0], T.sem[sem], T.sem.ls, ad[1], ad[0], sum(1 << e for e in es))
+        count["ls"] += len(es)
+
+    dma("a", "l_req", b("reqi"), hbm(T.req))
+    for h in (0, 1):
+        dma("s", "l_rec%d" % h, b("reci", 1024 * h, 1024 * h + 1024), (T.rec[:, 1024 * h:1024 * h + 1024], None, 0, 0))
+    dma("s", "l_wt", b("wtb"), hbm(T.wt))
+    dma("s", "l_aim", b("aimb"), hbm(T.aim))
+    dma("s", "l_mul", b("muli"), hbm(T.mul))
+    dma("s", "l_th", b("thi"), hbm(T.th))
+
+    iota(b("p8"), [[0, 128]], 8)
+    iota(b("pb"), [[1, 8], [128, 16]], 0)
+    fill(b("ones"), 1.0)
+    o128 = b("ones", 0, 128)
+    affine(b("bt"), o128, [[-16, 8], [0, 16]], A.is_ge, 0, 1)
+    affine(b("bo"), b("bt"), [[16, 8], [0, 16]], A.is_ge, 15, -1)
+    affine(b("idb"), o128, [[-1, 128]], A.is_equal, 0, 1)
+    for h in (0, 1):
+        affine(b("en", 1024 * h, 1024 * h + 1024), b("ones"), [[-1, 64], [0, 16]], A.is_equal, -64 * h, 1)
+    for r in range(16):
+        affine(sel(r), b("bo"), [[0, 8], [1, 16]], A.is_equal, -r, 0)
+
+    def gzero(lo, hi):
+        z = b("vz", 16 * lo, 16 * hi)
+        op("g", [lambda: g.iota(z[0], [[0, 16 * (hi - lo)]], 0, 0, allow_small_or_imprecise_dtypes=True)], [z], [])
+    for c, (lo, hi) in enumerate(CHUNKS):
+        if JUDGE[c] == "V":
+            gzero(lo, hi)
+    tsc(b("pa"), b("p8"), 127, A.bitwise_and)
+    tt(b("pc"), b("pa"), b("pb"), A.add)
+    copy(b("pm"), b("pc"))
+    tsc(b("ic"), b("pc", 0, 16), 0.125, A.mult)
+    copy(b("ic8"), b("pc", 0, 16))
+    tsc(b("ocol"), b("pc", 0, 1), 0.25, A.mult, 1.0, A.add)
+    fill(b("rm"), 1.0)
+    fill(b("rm", 0, WID, 16), 0.0)
+    fill(b("nb"), 0.0)
+    fill(b("nb", 0, WID, 16), BIG)
+
+    def zero(name, lo, hi):
+        for k in range(lo, hi, 1024):
+            m = min(1024, hi - k)
+            act(b(name, k, k + m), b("ones", 0, m), F.Copy, scale=0.0)
+    for c, (lo, hi) in enumerate(CHUNKS):
+        if NAMES[c] == "V":
+            zero("kz", 16 * lo, 16 * hi)
+    act(b("idh"), b("idb"), F.Copy)
+    act(b("nidb"), b("idb"), F.Copy, scale=-1.0)
+    act(b("hid"), b("idb"), F.Copy, scale=0.5)
+    act(b("mhalf"), o128, F.Copy, scale=-0.5)
+
+    def tail(src):
+        tsc(b("ki"), src, 7, A.bitwise_and)
+        tsc(b("ni"), src, 3, A.logical_shift_right, 255, A.bitwise_and)
+        tsc(b("k5"), b("ki"), 512.0, A.mult)
+        tt(b("pf"), b("k5"), b("ni"), A.add)
+        copy(b("cl"), b("pf"))
+        act(b("pfm"), b("pf"), F.Identity, bias=-255.0)
+
+    def kspread(c):
+        lo, hi = CHUNKS[c]
+        copy(b("kz", 16 * lo, 16 * hi, 16), b("k5", lo, hi))
+        scan(b("kb", 16 * lo, 16 * hi), b("rm", 0, 16 * (hi - lo)), b("kz", 16 * lo, 16 * hi), A.mult, A.add)
+
+    def trans(dst, src, h, o):
+        k = o + 128 * h
+        op("p", [lambda: P.transpose(T.psT[:, k:k + 128], b(src, 128 * h, 128 * h + 128)[0], T.idb[:])],
+           [b("psT", k, k + 128)], [b(src, 128 * h, 128 * h + 128), b("idb")])
+        act(b(dst, 128 * h, 128 * h + 128), b("psT", k, k + 128), F.Copy, scale=-1.0)
+
+    pend, pcount = [], [0]
+
+    def flush(keep=0):
+        while len(pend) > keep:
+            pend.pop(0)()
+
+    def psub(m, tname, data, ident, sink):
+        h, k, s = 128 * (m // 128), 16 * (m % 128), 512 * (pcount[0] % 2)
+        pcount[0] += 1
+        p = b("psS", s, s + 512)
+        mms(p, [(b(ident), data), (b(tname, h, h + 128), b("en", k, k + 512))])
+        pend.append(lambda: sink(p))
+        flush(1)
+
+    def ab4(lo, hi): return (T.ab[:, lo // 16:hi // 16, :, :], "ab", 16 * lo, 16 * hi)
+
+    tail(b("reqi"))
+    for c in range(nc):
+        if NAMES[c] == "V":
+            kspread(c)
+    for h in (0, 1):
+        lo, hi = 1024 * h, 1024 * h + 1024
+        tsc(b("ra", lo, hi), b("reci", lo, hi), 2047, A.bitwise_and)
+        tsc(b("rb", lo, hi), b("ra", lo, hi), 512.125, A.mult, -0.4375, A.add)
+    for k in range(8):
+        tsc(b("dw", 512 * k, 512 * k + 256), b("rb", k, 2048, 8), 3839, A.bitwise_and)
+    gact(b("xt"), b("reci"), b("pm"), F.Identity, bias=-1023.5 / 2048, scale=1.0 / 2048)
+    act(b("bo32"), b("bo"), F.Copy)
+    act(b("odd"), b("idb"), F.Copy, scale=b("ocol"))
+
+    def late():
+        for k in range(8):
+            tsc(b("xw", 512 * k, 512 * k + 256), b("xt", 256 * k, 256 * k + 256), ROUND, A.add, ROUND, A.subtract)
+        copy(b("kcol"), b("muli"))
+        copy(b("tcol"), b("thi"))
+
+    DW, XW = b("dw"), b("xw")
+    for t in range(STEPS):
+        last = t == STEPS - 1
+        CP, VV, PL, ACP, AV, APL = "cp%d" % t, "vv%d" % t, "pl%d" % t, "acp%d" % t, "av%d" % t, "apl%d" % t
+
+        def names_v(c, lo, hi):
+            gtt(b("xb", 16 * lo, 16 * hi), DW, b("cl", lo, hi), b("kb", 16 * lo, 16 * hi), A.subtract)
+
+        def names_abs(c, lo, hi):
+            act(b("yb", 16 * lo, 16 * hi), b("xb", 16 * lo, 16 * hi), F.Abs, bias=-255.0)
+
+        def names_a(c, lo, hi):
+            for m in range(lo, hi, 32):
+                w = b("xh", 16 * m, 16 * m + 512)
+                gact(w, DW, b("cl", m, m + 32), F.Identity, bias=-2048.0)
+                psub(m, "kt", w, "idh", lambda p, m=m: act(b("yb", 16 * m, 16 * m + 512), p, F.Abs, bias=1793.0))
+
+        def least(c, lo, hi):
+            flush()
+            w = (16 * lo, 16 * hi)
+            scan(b("sc", *w), b("nb", 0, 16 * (hi - lo)), b("yb", *w), A.max, A.min)
+            mms(b("psN", lo, hi), [(b("idb"), b("k5", lo, hi)), (b("nidb"), b("sc", 16 * lo + 15, 16 * hi, 16))])
+
+        def raised(c, lo, hi):
+            tt(b("mm", lo, hi), b("psN", lo, hi), b("pfm", lo, hi), A.max)
+            tsc(b(CP, lo, hi), b("mm", lo, hi), 255.0, A.add)
+            send(t, ACP, CP, "rc%d_%d" % (t, c), lo, hi)
+
+        def values(c, lo, hi):
+            gact(b("xg", 16 * lo, 16 * hi), XW, b(CP, lo, hi), F.Copy)
+
+        def extremes(c, lo, hi):
+            w, e = (16 * lo, 16 * hi), (16 * lo + 15, 16 * hi, 16)
+            scan(b("mx", *w), b("rm", 0, 16 * (hi - lo)), b("xg", *w), A.mult, A.max)
+            scan(b("mn", *w), b("nb", 0, 16 * (hi - lo)), b("xg", *w), A.max, A.min)
+            mms(b("psE", lo, hi), [(b("hid"), b("mx", *e)), (b("hid"), b("mn", *e)), (b("hid"), b("mhalf", 0, hi - lo))])
+
+        def halved(c, lo, hi):
+            tsc(b("zb", lo, hi), b("psE", lo, hi), ROUND, A.add, ROUND, A.subtract)
+            tt(b("zw", lo, hi), b("zb", lo, hi), b("wtb", lo, hi), A.mult)
+            mms(b("psV", lo, hi), [(b("idb"), b("zb", lo, hi)), (b("nidb"), b("aimb", lo, hi))])
+            act(b(VV, lo, hi), b("psV", lo, hi), F.Abs)
+            send(t, AV, VV, "rv%d_%d" % (t, c), lo, hi)
+            mms(b("psU", lo, hi), [(b("bo32"), b("zw", lo, hi))])
+
+        def places_sum(i, lo, hi):
+            q0, q1 = lo // 16, hi // 16
+            copy(b("ui", lo, hi), b("psU", lo, hi))
+            tsc(b("u7", lo, hi), b("ui", lo, hi), 7, A.bitwise_and)
+            tsc(b("u7b", lo, hi), b("u7", lo, hi), 32.0, A.mult)
+            mms(b("psP", q0, q1), [(sel(r), b("u7b", lo + r, hi, 16)) for r in range(16)] + [(b("idb"), b("ic", q0, q1))])
+
+        def places(i, lo, hi):
+            q0, q1 = lo // 16, hi // 16
+            copy(b("plu", q0, q1), b("psP", q0, q1))
+            if not last:
+                act(b(PL, q0, q1), b("psP", q0, q1), F.Copy)
+
+        def yz_out():
+            if last:
+                dma("s", "o_yz", hbm(T.yz), b("zb"))
+                tsc(b("u7c"), b("u7"), 0.0625, A.mult)
+                mms(b("psP", 32, 48), [(sel(r), b("u7c", r, 256, 16)) for r in range(16)] + [(b("idb"), b("ic8"))])
+                act(b(PL), b("psP", 32, 48), F.Copy)
+
+        def judge_v(c, lo, hi):
+            copy(b("vz", 16 * lo, 16 * hi, 16), b(AV, lo, hi))
+            scan(b("vb", 16 * lo, 16 * hi), b("rm", 0, 16 * (hi - lo)), b("vz", 16 * lo, 16 * hi), A.mult, A.add)
+            gtt(b("dg", 16 * lo, 16 * hi), XW, b(ACP, lo, hi), b("vb", 16 * lo, 16 * hi), A.subtract)
+
+        def judge_abs(c, lo, hi):
+            act(ab4(lo, hi), b("dg", 16 * lo, 16 * hi), F.Abs)
+
+        def judge_a(c, lo, hi):
+            for m in range(lo, hi, 32):
+                w = b("gx", 16 * m, 16 * m + 512)
+                gact(w, XW, b(ACP, m, m + 32), F.Copy)
+                psub(m, "vt", w, "idb", lambda p, m=m: act(ab4(m, m + 32), p, F.Abs))
+
+        def esum(c, lo, hi):
+            flush()
+            mms(b("psE", lo, hi), [(sel(r), (T.ab[:, lo // 16:hi // 16, r, :], "ab", 16 * lo, 16 * hi)) for r in range(16)])
+
+        def verdict(i, lo, hi):
+            q0, q1 = lo // 16, hi // 16
+            tsc(b("okm", lo, hi), b("psE", lo, hi), b("tcol"), A.is_lt)
+            scan(b("cnt", lo, hi), b("rm", 0, hi - lo), b("okm", lo, hi), A.mult, A.add)
+            tsc(b("t1", q0, q1), b("cnt", lo + 15, hi, 16), 6.5, A.is_lt, 2048.0 if last else 256.0, A.mult)
+            tt(b("t2", q0, q1), b("t1", q0, q1), b(APL, q0, q1), A.add)
+            if last:
+                tsc(b("off", q0, q1), b("t2", q0, q1), -8.0 * lo, A.add)
+            else:
+                copy(b("off", q0, q1), b("t2", q0, q1))
+
+        def nextreq():
+            mms(b("psU", 256, 512), [(b("odd"), b("zb"))])
+            tsc(b("uu"), b("ui"), 4095, A.bitwise_and)
+            tt(b("sq"), b("uu"), b("uu"), A.mult)
+            tsc(b("sh"), b("sq"), 5, A.logical_shift_right)
+            tsc(b("psN", 0, 256), b("uu"), b("kcol"), A.mult)
+            tt(b("s1"), b("sh"), b("psN", 0, 256), A.add)
+            tt(b("s2"), b("s1"), b("psU", 256, 512), A.add)
+            if last:
+                tsc(b("cr"), b("s2"), 2047, A.bitwise_and)
+                copy(b("yco"), b("cr"))
+                dma("s", "o_yc", hbm(T.yc), b("yco"))
+
+        def arrive_x():
+            if t == 0:
+                late()
+            else:
+                put(XW, b("off"), b("av%d" % (t - 1)))
+
+        def yo_own():
+            for k in range(8):
+                act(b("yo", k, 2048, 8), b("xw", 512 * k, 512 * k + 256), F.Copy)
+
+        def final(i, lo, hi):
+            put(b("yo", 8 * lo, 8 * hi + 2048), b("off", lo // 16, hi // 16), b(AV, lo, hi))
+            dma("s", "o_yx%d" % i, (T.yx[:, 8 * lo:8 * hi], None, 0, 0), b("yo", 8 * lo, 8 * hi))
+
+        BYCHUNK = {"n": names_v, "b": names_abs, "A": names_a, "r": least, "s": raised, "g": values, "h": extremes, "i": halved,
+                   "j": judge_v, "k": judge_abs, "J": judge_a, "e": esum, "K": lambda c, lo, hi: kspread(c)}
+        BYPART = {"p": places_sum, "q": places, "v": verdict, "E": final,
+                  "x": lambda i, lo, hi: put(XW, b("plu", lo // 16, hi // 16), b(VV, lo, hi)),
+                  "d": lambda i, lo, hi: put(DW, b("plu", lo // 16, hi // 16), b(CP, lo, hi)),
+                  "D": lambda i, lo, hi: put(DW, b("off", lo // 16, hi // 16), b(ACP, lo, hi))}
+        ONCE = {"X": arrive_x, "N": nextreq, "L": lambda: tail(b("s2")), "Y": yo_own, "Z": yz_out,
+                "P": lambda: send(t, APL, PL, "rp%d" % t, 0, 16)}
+        for tok in (SCHEDL if last else SCHED).split():
+            k, i = tok[0], int(tok[1:] or 0)
+            if k in BYCHUNK:
+                BYCHUNK[k](i, *CHUNKS[i])
+            elif k in BYPART:
+                BYPART[k](i, *PARTS[i])
+            elif k == "U":
+                trans("kt", "k5", i, 0)
+            elif k == "T":
+                trans("vt", AV, i, 256)
+            else:
+                ONCE[k]()
+    for s in sorted(count):
+        g.wait_ge(T.sem[s], count[s])

@@ -3,37 +3,42 @@ from concourse.mybir import AluOpType, ActivationFunctionType
 A = AluOpType
 F = ActivationFunctionType
 STEPS = 3
-CHUNKS = [(0, 64), (64, 128), (128, 192), (192, 256)]
-PARTS = [(0, 192), (192, 256)]
-NAMES = "AVAV"
-JUDGE = "AAVV"
-SCHED = ("X n1 U1 U0 A0 A2 b1 r0 n3 s0 r1 g0 r2 s1 g1 b3 s2 h0 h1 g2 r3 i0 s3 i1 h2 g3 i2 p0 h3 i3 q0 p1 x0 q1 T0 x1 "
-         "J0 j2 k2 Z N e2 d1 P j3 J1 e0 d0 k3 e1 L v0 D0 e3 v1 D1 K1 K3")
-SCHEDL = ("X n1 U1 U0 A0 A2 b1 r0 n3 s0 r1 g0 r2 s1 g1 b3 s2 h0 h1 g2 r3 i0 s3 i1 h2 g3 i2 p0 h3 i3 q0 p1 x0 q1 T0 x1 "
-          "J0 j2 k2 Z N e2 P j3 J1 e0 Y k3 e1 v0 e3 E0 v1 E1")
-BIG = 16384.0
+READ = "X A02 102 A58 B02 n25 r02 R02 b25 168 156 A8a 18a Aad r25 g02 1ac B58 B8a 1cd Bad R25 h02 g25 r58 O58 r8a W Adg rad 1de I02 Oad O8a Gad 1eg g58 h25 h58 Bdg I25 a25 a02 Had rdg Iad I58 g8a Odg c05 Gdg z02 h8a z25 z58 cad I8a z8a a58 c5a a8a p0a aad Hdg zad idg Zdg V adg q0a x0a s05 u y pag qag s5a S sad sdg cdg xag P"
+SCHED = READ + " T0 J04 j8b J48 N 202 224 T1 k04 246 w8b jbe m8b 268 k48 wbe e8b Jeg e08 mbe 2eg L keg v08 ebe d0g eeg l K25 U1 U0 D08 v8g D8g M"
+SCHEDL = READ + " T0 J48 268 J04 246 T1 k48 202 224 k04 N j8b jbe wbe mbe ebe w8b F Y m8b C e08 Jeg 2eg v08 e8b E08 v8e E8e keg eeg veg Eeg"
+BIG = 8192.0
 ROUND = 12582912.0
-WID = 16 * max(hi - lo for lo, hi in CHUNKS)
+ROUND4096 = ROUND * 4096
+WID = 1024
 
-SCRATCH = {"psS": ("psum", [128, 1024], "float32"), "psV": ("psum", [128, 512], "float32"), "psE": ("psum", [128, 512], "float32"),
-           "psU": ("psum", [128, 512], "float32"), "psP": ("psum", [128, 512], "float32"), "psN": ("psum", [128, 512], "float32"),
-           "psT": ("psum", [128, 1024], "bfloat16"), "ab": ("sbuf", [128, 16, 16, 16], "bfloat16")}
+
+def tokens(s):
+    return [(k[0], 16 * int(k[1], 17), 16 * int(k[2], 17)) if len(k) == 3 else (k[0], int(k[1:] or 0), 0) for k in s.split()]
+
+
+SENDS = [k for k in tokens(READ) if k[0] in "cs"]
+SCRATCH = {"psS": ("psum", [128, 2048], "float32"), "psV": ("psum", [128, 512], "float32"), "psE": ("psum", [128, 512], "float32"),
+           "psP": ("psum", [128, 512], "float32"), "psN": ("psum", [128, 512], "float32"),
+           "ab": ("sbuf", [128, 16, 256], "bfloat16"), "dg": ("sbuf", [128, 16, 256], "bfloat16")}
 for _d, _w, _names in (
-        ("int32", 4096, "dw"), ("bfloat16", 4096, "xw yo"), ("int32", 2048, "reci ra rb"), ("float32", 2048, "xt"),
-        ("int32", 1, "muli thi"), ("float32", 1, "kcol tcol ocol"), ("int32", 128, "p8 pa pb pc"), ("uint16", 128, "pm"),
-        ("int32", 256, "reqi ni ki ui u7 uu sq sh s1 s2 cr"), ("bfloat16", 256, "aimb wtb k5 kt vt zb u7b u7c okm cnt"),
-        ("float32", 256, "pf pfm mm zw yco"), ("uint16", 256, "cl"), ("float32", 128, "bo32"),
-        ("bfloat16", 128, "bt bo idb nidb hid mhalf odd"), ("float16", 128, "idh"), ("bfloat16", 1024, "ones"),
-        ("bfloat16", 2048, "en sel"), ("bfloat16", WID, "nb rm"), ("bfloat16", 16, "ic ic8"), ("float32", 16, "t1 t2"),
-        ("uint16", 16, "plu off"), ("bfloat16", 4096, "kz kb vz vb xb yb sc xg mx mn dg gx"), ("float16", 4096, "xh")):
+        ("int32", 4096, "dw"), ("bfloat16", 4096, "xw yo"), ("int32", 2048, "reci ra rb"), ("float16", 2048, "xt"),
+        ("int32", 1, "muli thi"), ("float32", 1, "kcol tcol ocol ocol2"), ("int32", 16, "p8 pa pb pc pi p9"),
+        ("int32", 256, "reqi ni ki sh s2 cr"), ("bfloat16", 256, "aimb wtb cw nk nib mm mid hq kt vt zc zo okm cnt offc"),
+        ("float32", 256, "sq yco"), ("float16", 256, "zw zb aimc uc"), ("uint16", 256, "cl"),
+        ("bfloat16", 128, "bt bo idb nidb big mhalf odd odd2"), ("float16", 128, "idh hid dk"), ("bfloat16", 1024, "ones"),
+        ("bfloat16", 2048, "en sel"), ("bfloat16", WID, "nb rm xoff"), ("bfloat16", 16, "ic"), ("float32", 16, "t1 t2 ic8"),
+        ("uint16", 16, "plu off"), ("bfloat16", 4096, "kz kb vz vb gx yb sc"), ("float16", 4096, "xh xb xg mxa mna"),
+        ("float16", 2048, "mx mn")):
     for _n in _names.split():
         SCRATCH[_n] = ("sbuf", [128, _w], _d)
 for _t in range(STEPS):
-    for _n, _w, _d in (("cp", 256, "uint16"), ("vv", 256, "bfloat16"), ("pl", 16, "float32")):
+    for _n, _w, _d in (("cp", 256, "uint16"), ("vv", 256, "bfloat16"), ("pl", 16, "int32")):
         SCRATCH["%s%d" % (_n, _t)] = SCRATCH["a%s%d" % (_n.replace("vv", "v"), _t)] = ("sbuf", [128, _w], _d)
-SEMAPHORES = ["sv", "sa", "sp", "sg", "ls", "l_req", "l_aim", "l_wt", "l_mul", "l_th", "l_rec0", "l_rec1", "o_yc", "o_yz", "o_yx0", "o_yx1"]
+LOADS = 4
+SEMAPHORES = ["sv", "sa", "sp", "sg", "ls", "l_req", "l_aim", "l_wt", "l_mul", "l_th", "o_yc", "o_yz"]
+SEMAPHORES += ["l_rec%d" % _h for _h in range(LOADS)] + ["o_yx%d" % _k[1] for _k in tokens(SCHEDL) if _k[0] == "E"]
 for _t in range(STEPS):
-    SEMAPHORES += ["rp%d" % _t] + ["r%s%d_%d" % (_x, _t, _c) for _x in "cv" for _c in range(len(CHUNKS))]
+    SEMAPHORES += ["rp%d" % _t] + ["r%s%d_%d" % (_k[0], _t, _k[1]) for _k in SENDS]
 
 
 def tracker(g, T):
@@ -73,15 +78,14 @@ def tracker(g, T):
         for lst, isw in ((ins, False), (outs, True)):
             for (_, name, lo, hi) in lst:
                 h = hist.setdefault(name, [])
-                if isw and name[:2] != "ps":
-                    h[:] = [e for e in h if not (lo <= e[0] and e[1] <= hi)]
-                else:
-                    h[:] = [e for e in h if not (e[0] == lo and e[1] == hi and e[2] == q and e[5] == isw)]
+                h[:] = [e for e in h if not (e[0] == lo and e[1] == hi and e[2] == q and e[5] == isw)]
                 h.append((lo, hi, q, src, n, isw))
 
-    def op(q, calls, outs, ins):
-        need(q, outs, ins)
-        for c in calls:
+    def op(q, calls, outs, ins, each=None):
+        need(q, outs, [] if each else ins)
+        for j, c in enumerate(calls):
+            if each:
+                need(q, [], each[j])
             i = c()
         s = SEM[q]
         i.then_inc(T.sem[s], 1)
@@ -105,7 +109,6 @@ def rank_program(g, core, T, topo):
     op, dma, need, note, count = tracker(g, T)
     V, S, P = g.vector, g.scalar, g.tensor
     N = len(T.cores)
-    nc = len(CHUNKS)
 
     def b(name, lo=0, hi=None, st=1):
         w = T[name].shape[1]
@@ -113,6 +116,13 @@ def rank_program(g, core, T, topo):
         if lo == 0 and hi == w and st == 1:
             return (T[name][:], name, lo, hi)
         return (T[name][:, lo:hi:st] if st > 1 else T[name][:, lo:hi], name, lo, hi)
+
+    def back(name, lo, hi, st=1):
+        return (T[name][:, hi - 1:(lo - 1 if lo else None):-st], name, lo, hi)
+
+    def four(name, lo, hi, r=None):
+        t = T[name]
+        return (t[:, lo // 16:hi // 16, :] if r is None else t[:, lo // 16:hi // 16, 16 * r:16 * r + 16], name, 16 * lo, 16 * hi)
 
     def hbm(t): return (t[:], None, 0, 0)
     def ind(win, off): return T[win[1]][:, win[2]:win[3]].indirect(off[0])
@@ -128,7 +138,7 @@ def rank_program(g, core, T, topo):
             op("v", [lambda: V.tensor_scalar(o[0], x[0], va, a2, f, f2)], [o], ins)
 
     def fill(o, c): op("v", [lambda: V.memset(o[0], c)], [o], [])
-    def scan(o, d0, d1, f0, f1): op("v", [lambda: V.tensor_tensor_scan(o[0], d0[0], d1[0], 0.0, f0, f1)], [o], [d0, d1])
+    def scan(o, d0, d1, f0, f1, first=0.0): op("v", [lambda: V.tensor_tensor_scan(o[0], d0[0], d1[0], first, f0, f1)], [o], [d0, d1])
 
     def act(o, i, f, bias=0.0, scale=1.0):
         col = [scale] if isinstance(scale, tuple) else []
@@ -141,22 +151,23 @@ def rank_program(g, core, T, topo):
     def gtt(o, win, off, y, f): op("v", [lambda: V.tensor_tensor(o[0], ind(win, off), y[0], f)], [o], [win, off, y])
     def put(win, off, val): op("v", [lambda: V.tensor_copy(ind(win, off), val[0])], [win], [off, val])
     def affine(o, i, pat, f, base, cm): op("g", [lambda: g.affine_select(o[0], i[0], pat, f, 0.0, base, cm)], [o], [i])
-    def iota(o, pat, cm): op("g", [lambda: g.iota(o[0], pat, 0, cm)], [o], [])
+
+    def iota(o, pat, base, cm):
+        op("g", [lambda: g.iota(o[0], pat, base, cm, allow_small_or_imprecise_dtypes=True)], [o], [])
 
     def mms(o, terms):
         k = len(terms) - 1
         op("p", [lambda j=j, l=l, r=r: P.matmul(o[0], l[0], r[0], j == 0, j == k) for j, (l, r) in enumerate(terms)],
-           [o], [x for t in terms for x in t])
+           [o], [x for t in terms for x in t], terms)
 
     def sel(r): return b("sel", 128 * r, 128 * r + 128)
 
     def eng(src, dst): return topo.engines(src, dst)[:8]
     for t in range(STEPS):
         n = len(eng(T.cores[(rank - 1 - t) % N], core))
-        for c, (lo, hi) in enumerate(CHUNKS):
-            for x, nm in (("c", "acp%d"), ("v", "av%d")):
-                note("r", "r%s%d_%d" % (x, t, c), n, [b(nm % t, lo, hi)], [])
-                count["r%s%d_%d" % (x, t, c)] = n
+        for x, lo, hi in SENDS:
+            note("r", "r%s%d_%d" % (x, t, lo), n, [b(("acp%d" if x == "c" else "av%d") % t, lo, hi)], [])
+            count["r%s%d_%d" % (x, t, lo)] = n
         note("r", "rp%d" % t, n, [b("apl%d" % t)], [])
         count["rp%d" % t] = n
     count["ls"] = 0
@@ -170,195 +181,220 @@ def rank_program(g, core, T, topo):
         count["ls"] += len(es)
 
     dma("a", "l_req", b("reqi"), hbm(T.req))
-    for h in (0, 1):
-        dma("s", "l_rec%d" % h, b("reci", 1024 * h, 1024 * h + 1024), (T.rec[:, 1024 * h:1024 * h + 1024], None, 0, 0))
-    dma("s", "l_wt", b("wtb"), hbm(T.wt))
-    dma("s", "l_aim", b("aimb"), hbm(T.aim))
+    LW = 2048 // LOADS
+    for h in range(LOADS):
+        dma("s", "l_rec%d" % h, b("reci", LW * h, LW * h + LW), (T.rec[:, LW * h:LW * h + LW], None, 0, 0))
     dma("s", "l_mul", b("muli"), hbm(T.mul))
     dma("s", "l_th", b("thi"), hbm(T.th))
+    dma("s", "l_aim", b("aimb"), hbm(T.aim))
+    dma("s", "l_wt", b("wtb"), hbm(T.wt))
 
-    iota(b("p8"), [[0, 128]], 8)
-    iota(b("pb"), [[1, 8], [128, 16]], 0)
     fill(b("ones"), 1.0)
     o128 = b("ones", 0, 128)
+    iota(b("p8"), [[0, 16]], 0, 1)
+    iota(b("pb"), [[16, 16]], 0, 0)
+    affine(b("idb"), o128, [[-1, 128]], A.is_equal, 0, 1)
+    affine(b("en", 0, 1024), b("ones", 0, 1024), [[-1, 64], [0, 16]], A.is_equal, 0, 1)
+    affine(b("en", 1024, 2048), b("ones", 0, 1024), [[-1, 64], [0, 16]], A.is_equal, -64, 1)
+    iota(b("xoff"), [[0, WID // 256], [256, 16], [0, 16]], -2048, 0)
+    iota((T.offc[0:64, :], "offc", 0, 256), [[0, 16], [-4, 16]], 32, 0)
     affine(b("bt"), o128, [[-16, 8], [0, 16]], A.is_ge, 0, 1)
     affine(b("bo"), b("bt"), [[16, 8], [0, 16]], A.is_ge, 15, -1)
-    affine(b("idb"), o128, [[-1, 128]], A.is_equal, 0, 1)
-    for h in (0, 1):
-        affine(b("en", 1024 * h, 1024 * h + 1024), b("ones"), [[-1, 64], [0, 16]], A.is_equal, -64 * h, 1)
     for r in range(16):
         affine(sel(r), b("bo"), [[0, 8], [1, 16]], A.is_equal, -r, 0)
-
-    def gzero(lo, hi):
-        z = b("vz", 16 * lo, 16 * hi)
-        op("g", [lambda: g.iota(z[0], [[0, 16 * (hi - lo)]], 0, 0, allow_small_or_imprecise_dtypes=True)], [z], [])
-    for c, (lo, hi) in enumerate(CHUNKS):
-        if JUDGE[c] == "V":
-            gzero(lo, hi)
-    tsc(b("pa"), b("p8"), 127, A.bitwise_and)
-    tt(b("pc"), b("pa"), b("pb"), A.add)
-    copy(b("pm"), b("pc"))
-    tsc(b("ic"), b("pc", 0, 16), 0.125, A.mult)
-    copy(b("ic8"), b("pc", 0, 16))
-    tsc(b("ocol"), b("pc", 0, 1), 0.25, A.mult, 1.0, A.add)
     fill(b("rm"), 1.0)
     fill(b("rm", 0, WID, 16), 0.0)
     fill(b("nb"), 0.0)
     fill(b("nb", 0, WID, 16), BIG)
-
-    def zero(name, lo, hi):
-        for k in range(lo, hi, 1024):
-            m = min(1024, hi - k)
-            act(b(name, k, k + m), b("ones", 0, m), F.Copy, scale=0.0)
-    for c, (lo, hi) in enumerate(CHUNKS):
-        if NAMES[c] == "V":
-            zero("kz", 16 * lo, 16 * hi)
+    fill(b("mhalf"), -0.5)
+    for x, lo, hi in tokens(SCHED):
+        if x == "K":
+            fill(b("kz", 16 * lo, 16 * hi), 0.0)
+    tsc(b("pa"), b("p8"), 15, A.bitwise_and)
+    tt(b("pc"), b("pa"), b("pb"), A.add)
     act(b("idh"), b("idb"), F.Copy)
     act(b("nidb"), b("idb"), F.Copy, scale=-1.0)
-    act(b("hid"), b("idb"), F.Copy, scale=0.5)
-    act(b("mhalf"), o128, F.Copy, scale=-0.5)
 
-    def tail(src):
-        tsc(b("ki"), src, 7, A.bitwise_and)
-        tsc(b("ni"), src, 3, A.logical_shift_right, 255, A.bitwise_and)
-        tsc(b("k5"), b("ki"), 512.0, A.mult)
-        tt(b("pf"), b("k5"), b("ni"), A.add)
-        copy(b("cl"), b("pf"))
-        act(b("pfm"), b("pf"), F.Identity, bias=-255.0)
+    def split(src="s2"):
+        tsc(b("ki"), b(src), 7, A.bitwise_and)
+        tsc(b("ni"), b(src), 3, A.arith_shift_right, 255, A.bitwise_and)
 
-    def kspread(c):
-        lo, hi = CHUNKS[c]
-        copy(b("kz", 16 * lo, 16 * hi, 16), b("k5", lo, hi))
+    def keyed(plain=False):
+        act(b("nk"), b("ki"), F.Identity, scale=-512.0 if plain else 512.0, bias=1536.0 if plain else -2048.0)
+        act(b("nib"), b("ni"), F.Identity, scale=-1.0 if plain else 1.0, bias=255.0 if plain else 0.0)
+        mms(b("psN", 0, 256), [(b("nidb"), b("nk")), (b("nidb"), b("nib"))])
+
+    def listed():
+        act(b("cl"), b("psN", 0, 256), F.Identity, bias=1791.0)
+
+    def kspread(lo, hi):
+        copy(b("kz", 16 * lo, 16 * hi, 16), b("nk", lo, hi))
         scan(b("kb", 16 * lo, 16 * hi), b("rm", 0, 16 * (hi - lo)), b("kz", 16 * lo, 16 * hi), A.mult, A.add)
 
-    def trans(dst, src, h, o):
-        k = o + 128 * h
-        op("p", [lambda: P.transpose(T.psT[:, k:k + 128], b(src, 128 * h, 128 * h + 128)[0], T.idb[:])],
-           [b("psT", k, k + 128)], [b(src, 128 * h, 128 * h + 128), b("idb")])
-        act(b(dst, 128 * h, 128 * h + 128), b("psT", k, k + 128), F.Copy, scale=-1.0)
+    def trans(dst, src, h, scale):
+        k = 256 + 128 * h
+        mms(b("psV", k, k + 128), [(src, b("idb"))])
+        act(b(dst, 128 * h, 128 * h + 128), b("psV", k, k + 128), F.Copy, scale=scale)
 
-    pend, pcount = [], [0]
+    def keys_t(h): trans("kt", b("nk", 128 * h, 128 * h + 128), h, 1.0)
+    def ring(lo, hi): return b("psS", 16 * lo % 2048, 16 * lo % 2048 + 16 * (hi - lo))
 
-    def flush(keep=0):
-        while len(pend) > keep:
-            pend.pop(0)()
+    def psub(lo, hi, tname, data, ident):
+        cuts = [lo] + [m for m in range(0, 256, 32) if lo < m < hi] + [hi]
+        for m, e in zip(cuts, cuts[1:]):
+            h, k = 128 * (m // 128), 16 * (m % 128)
+            mms(ring(m, e), [(b(tname, h, h + 128), b("en", k, k + 16 * (e - m))), (b(ident), b(data, 16 * m, 16 * e))])
 
-    def psub(m, tname, data, ident, sink):
-        h, k, s = 128 * (m // 128), 16 * (m % 128), 512 * (pcount[0] % 2)
-        pcount[0] += 1
-        p = b("psS", s, s + 512)
-        mms(p, [(b(ident), data), (b(tname, h, h + 128), b("en", k, k + 512))])
-        pend.append(lambda: sink(p))
-        flush(1)
+    def low(h): tsc(b("ra", LW * h, LW * h + LW), b("reci", LW * h, LW * h + LW), 2047, A.bitwise_and)
+    def wide(h): act(b("rb", LW * h, LW * h + LW), b("ra", LW * h, LW * h + LW), F.Identity, scale=512.125, bias=-0.4375)
 
-    def ab4(lo, hi): return (T.ab[:, lo // 16:hi // 16, :, :], "ab", 16 * lo, 16 * hi)
+    def high(h):
+        act(b("xt", LW * h, LW * h + LW), b("reci", LW * h, LW * h + LW), F.Identity, bias=1279.5 + 1.0 / 4096, scale=1.0 / 2048)
 
-    tail(b("reqi"))
-    for c in range(nc):
-        if NAMES[c] == "V":
-            kspread(c)
-    for h in (0, 1):
-        lo, hi = 1024 * h, 1024 * h + 1024
-        tsc(b("ra", lo, hi), b("reci", lo, hi), 2047, A.bitwise_and)
-        tsc(b("rb", lo, hi), b("ra", lo, hi), 512.125, A.mult, -0.4375, A.add)
-    for k in range(8):
-        tsc(b("dw", 512 * k, 512 * k + 256), b("rb", k, 2048, 8), 3839, A.bitwise_and)
-    gact(b("xt"), b("reci"), b("pm"), F.Identity, bias=-1023.5 / 2048, scale=1.0 / 2048)
-    act(b("bo32"), b("bo"), F.Copy)
-    act(b("odd"), b("idb"), F.Copy, scale=b("ocol"))
+    def names(h):
+        for k in range(8):
+            c = 512 * k + 128 * h
+            tsc(b("dw", c, c + 128), b("rb", 1024 * h + k, 1024 * h + 1024, 8), 3839, A.bitwise_and)
+    split("reqi")
+    keyed(True)
+    low(0), wide(0), listed()
+    tsc(b("ic"), b("pc"), 1.0 / 512, A.mult)
+    tsc(b("ic8"), b("pc"), 8.0, A.mult)
+    tsc(b("ocol"), b("pa", 0, 1), -2.0, A.mult, -1.0, A.add)
+    tsc(b("ocol2"), b("pa", 0, 1), 2560.0, A.mult, 1280.0, A.add)
+    low(1), wide(1), keys_t(0), keys_t(1), high(0)
+    for x, lo, hi in tokens(SCHED):
+        if x == "K":
+            kspread(lo, hi)
+    low(2), wide(2), high(1), names(0), low(3), wide(3), high(2), high(3)
+    tsc(b("kcol"), b("muli"), -1.0, A.mult, 1920.0, A.add)
+    copy(b("tcol"), b("thi"))
+    fill((T.offc[64:128, :], "offc", 0, 256), -1.0 / 256)
+    names(1)
+    act(b("hid"), b("idb"), F.Copy, scale=0.5)
 
     def late():
         for k in range(8):
-            tsc(b("xw", 512 * k, 512 * k + 256), b("xt", 256 * k, 256 * k + 256), ROUND, A.add, ROUND, A.subtract)
-        copy(b("kcol"), b("muli"))
-        copy(b("tcol"), b("thi"))
+            tsc(b("xw", 512 * k, 512 * k + 256), b("xt", k, 2048, 8), -1280.0, A.add)
+
+    def later():
+        act(b("aimc"), b("aimb"), F.Identity, scale=-1.0, bias=-1280.0)
+        act(b("mid"), b("ones", 0, 256), F.Copy, scale=-1408.0)
+
+    def latest():
+        act(b("cw"), b("wtb"), F.Identity, scale=128.0, bias=-128.0)
+        act(b("big"), b("idb"), F.Copy, scale=-4096.0)
+        act(b("dk"), b("idb"), F.Copy, scale=b("kcol"))
+        act(b("odd"), b("idb"), F.Copy, scale=b("ocol"))
+        act(b("odd2"), b("idb"), F.Copy, scale=b("ocol2"))
+        spread = [k for k in tokens(SCHED + " " + SCHEDL) if k[0] == "j"]
+        lo, hi = min(k[1] for k in spread), max(k[2] for k in spread)
+        iota(b("vz", 16 * lo, 16 * hi), [[0, 16 * (hi - lo)]], 0, 0)
 
     DW, XW = b("dw"), b("xw")
     for t in range(STEPS):
         last = t == STEPS - 1
         CP, VV, PL, ACP, AV, APL = "cp%d" % t, "vv%d" % t, "pl%d" % t, "acp%d" % t, "av%d" % t, "apl%d" % t
+        folded, toks = set(), set(tokens(READ))
 
-        def names_v(c, lo, hi):
-            gtt(b("xb", 16 * lo, 16 * hi), DW, b("cl", lo, hi), b("kb", 16 * lo, 16 * hi), A.subtract)
+        def names_v(lo, hi):
+            gtt(b("xb", 16 * lo, 16 * hi), DW, b("cl", lo, hi), b("kb", 16 * lo, 16 * hi), A.add)
 
-        def names_abs(c, lo, hi):
-            act(b("yb", 16 * lo, 16 * hi), b("xb", 16 * lo, 16 * hi), F.Abs, bias=-255.0)
+        def names_abs(lo, hi):
+            act(b("yb", 16 * lo, 16 * hi), b("xb", 16 * lo, 16 * hi), F.Abs, bias=-1791.0)
 
-        def names_a(c, lo, hi):
-            for m in range(lo, hi, 32):
-                w = b("xh", 16 * m, 16 * m + 512)
-                gact(w, DW, b("cl", m, m + 32), F.Identity, bias=-2048.0)
-                psub(m, "kt", w, "idh", lambda p, m=m: act(b("yb", 16 * m, 16 * m + 512), p, F.Abs, bias=1793.0))
+        def names_a(lo, hi):
+            gact(b("xh", 16 * lo, 16 * hi), DW, b("cl", lo, hi), F.Identity, bias=-2048.0)
 
-        def least(c, lo, hi):
-            flush()
-            w = (16 * lo, 16 * hi)
-            scan(b("sc", *w), b("nb", 0, 16 * (hi - lo)), b("yb", *w), A.max, A.min)
-            mms(b("psN", lo, hi), [(b("idb"), b("k5", lo, hi)), (b("nidb"), b("sc", 16 * lo + 15, 16 * hi, 16))])
+        def names_ps(lo, hi):
+            act(b("yb", 16 * lo, 16 * hi), ring(lo, hi), F.Abs, bias=257.0)
 
-        def raised(c, lo, hi):
-            tt(b("mm", lo, hi), b("psN", lo, hi), b("pfm", lo, hi), A.max)
-            tsc(b(CP, lo, hi), b("mm", lo, hi), 255.0, A.add)
-            send(t, ACP, CP, "rc%d_%d" % (t, c), lo, hi)
+        def least(lo, hi):
+            scan(b("sc", 16 * lo, 16 * hi), b("nb", 0, 16 * (hi - lo)), b("yb", 16 * lo, 16 * hi), A.max, A.min)
+            tt(b("mm", lo, hi), b("sc", 16 * lo + 15, 16 * hi, 16), b("nib", lo, hi), A.min)
+            o = b("psP", 256 + lo, 256 + hi) if ("R", lo, hi) in toks else b("psN", lo, hi)
+            mms(o, [(b("nidb"), b("nk", lo, hi)), (b("nidb"), b("mm", lo, hi))])
 
-        def values(c, lo, hi):
+        def raised(lo, hi):
+            tsc(b(CP, lo, hi), b("psP", 256 + lo, 256 + hi), 1791.0, A.add)
+
+        def risen(lo, hi):
+            act(b(CP, lo, hi), b("psN", lo, hi), F.Identity, bias=1791.0)
+
+        def values_v(lo, hi):
+            gtt(b("xg", 16 * lo, 16 * hi), XW, b(CP, lo, hi), b("xoff", 0, 16 * (hi - lo)), A.add)
+
+        def extremes_v(lo, hi):
+            for m in range(16 * lo, 16 * hi, 256):
+                scan(b("mx", m // 2, m // 2 + 128), b("xg", m, m + 256, 2), b("xg", m + 1, m + 256, 2), A.max, A.max, -4096.0)
+            for m in range(16 * lo, 16 * hi, 256):
+                scan(back("mn", m // 2, m // 2 + 128), back("xg", m, m + 256, 2), back("xg", m, m + 255, 2), A.min, A.min, 4096.0)
+            mms(b("psE", lo, hi), [(o128, b("offc", lo, hi)), (b("hid"), b("mx", 8 * lo + 7, 8 * hi, 8)),
+                                   (b("hid"), b("mn", 8 * lo, 8 * hi, 8))])
+
+        def values_a(lo, hi):
             gact(b("xg", 16 * lo, 16 * hi), XW, b(CP, lo, hi), F.Copy)
 
-        def extremes(c, lo, hi):
+        def extremes_a(lo, hi):
             w, e = (16 * lo, 16 * hi), (16 * lo + 15, 16 * hi, 16)
-            scan(b("mx", *w), b("rm", 0, 16 * (hi - lo)), b("xg", *w), A.mult, A.max)
-            scan(b("mn", *w), b("nb", 0, 16 * (hi - lo)), b("xg", *w), A.max, A.min)
-            mms(b("psE", lo, hi), [(b("hid"), b("mx", *e)), (b("hid"), b("mn", *e)), (b("hid"), b("mhalf", 0, hi - lo))])
+            scan(b("mxa", *w), b("rm", 0, 16 * (hi - lo)), b("xg", *w), A.mult, A.max)
+            scan(b("mna", *w), b("nb", 0, 16 * (hi - lo)), b("xg", *w), A.max, A.min)
+            mms(b("psE", lo, hi), [(b("hid"), b("mhalf", 0, hi - lo)), (b("hid"), b("mxa", *e)), (b("hid"), b("mna", *e))])
 
-        def halved(c, lo, hi):
-            tsc(b("zb", lo, hi), b("psE", lo, hi), ROUND, A.add, ROUND, A.subtract)
-            tt(b("zw", lo, hi), b("zb", lo, hi), b("wtb", lo, hi), A.mult)
-            mms(b("psV", lo, hi), [(b("idb"), b("zb", lo, hi)), (b("nidb"), b("aimb", lo, hi))])
-            act(b(VV, lo, hi), b("psV", lo, hi), F.Abs)
-            send(t, AV, VV, "rv%d_%d" % (t, c), lo, hi)
-            mms(b("psU", lo, hi), [(b("bo32"), b("zw", lo, hi))])
+        def halved(lo, hi, scalar):
+            if scalar:
+                act(b("zb", lo, hi), b("psE", lo, hi), F.Identity, bias=1280.0)
+            else:
+                tsc(b("zb", lo, hi), b("psE", lo, hi), 1280.0, A.add)
+            if ("z", lo, hi) in toks:
+                mms(b("psP", 256 + lo, 256 + hi), [(b("idb"), b("mid", lo, hi)), (b("idh"), b("zb", lo, hi))])
+            mms(b("psV", lo, hi), [(b("idh"), b("aimc", lo, hi)), (b("idh"), b("zb", lo, hi))])
 
-        def places_sum(i, lo, hi):
+        def weigh(lo, hi):
+            tt(b("zw", lo, hi), b("psP", 256 + lo, 256 + hi), b("wtb", lo, hi), A.mult)
+
+        def weigh_v(lo, hi):
+            tsc(b("zc", lo, hi), b("zb", lo, hi), -1408.0, A.add)
+            tt(b("zw", lo, hi), b("zc", lo, hi), b("wtb", lo, hi), A.mult)
+
+        def places_sum(lo, hi):
             q0, q1 = lo // 16, hi // 16
-            copy(b("ui", lo, hi), b("psU", lo, hi))
-            tsc(b("u7", lo, hi), b("ui", lo, hi), 7, A.bitwise_and)
-            tsc(b("u7b", lo, hi), b("u7", lo, hi), 32.0, A.mult)
-            mms(b("psP", q0, q1), [(sel(r), b("u7b", lo + r, hi, 16)) for r in range(16)] + [(b("idb"), b("ic", q0, q1))])
+            mms(b("psP", q0, q1), [(b("idb"), b("ic", q0, q1))] + [(sel(r), b("zw", lo + r, hi, 16)) for r in range(16)])
 
-        def places(i, lo, hi):
+        def places(lo, hi):
             q0, q1 = lo // 16, hi // 16
-            copy(b("plu", q0, q1), b("psP", q0, q1))
-            if not last:
-                act(b(PL, q0, q1), b("psP", q0, q1), F.Copy)
+            tsc(b("pi", q0, q1), b("psP", q0, q1), 512.0, A.mult)
+            tsc(b("p9" if last else PL, q0, q1), b("pi", q0, q1), 3839, A.bitwise_and)
+            copy(b("plu", q0, q1), b("p9" if last else PL, q0, q1))
 
-        def yz_out():
+        def send_places():
             if last:
-                dma("s", "o_yz", hbm(T.yz), b("zb"))
-                tsc(b("u7c"), b("u7"), 0.0625, A.mult)
-                mms(b("psP", 32, 48), [(sel(r), b("u7c", r, 256, 16)) for r in range(16)] + [(b("idb"), b("ic8"))])
-                act(b(PL), b("psP", 32, 48), F.Copy)
+                tsc(b("pi"), b("p9"), 9, A.logical_shift_right)
+                tt(b(PL), b("pi"), b("ic8"), A.add)
+            send(t, APL, PL, "rp%d" % t, 0, 16)
 
-        def judge_v(c, lo, hi):
+        def spread_v(lo, hi):
             copy(b("vz", 16 * lo, 16 * hi, 16), b(AV, lo, hi))
             scan(b("vb", 16 * lo, 16 * hi), b("rm", 0, 16 * (hi - lo)), b("vz", 16 * lo, 16 * hi), A.mult, A.add)
-            gtt(b("dg", 16 * lo, 16 * hi), XW, b(ACP, lo, hi), b("vb", 16 * lo, 16 * hi), A.subtract)
 
-        def judge_abs(c, lo, hi):
-            act(ab4(lo, hi), b("dg", 16 * lo, 16 * hi), F.Abs)
+        def judge_v(lo, hi):
+            for m in range(lo, hi, 16):
+                gtt((T.dg[:, m // 16, :], "dg", 16 * m, 16 * m + 256), XW, b(ACP, m, m + 16), b("vb", 16 * m, 16 * m + 256), A.subtract)
 
-        def judge_a(c, lo, hi):
-            for m in range(lo, hi, 32):
-                w = b("gx", 16 * m, 16 * m + 512)
-                gact(w, XW, b(ACP, m, m + 32), F.Copy)
-                psub(m, "vt", w, "idb", lambda p, m=m: act(ab4(m, m + 32), p, F.Abs))
+        def judge_fold(lo, hi):
+            tsc(four("ab", lo, hi), four("dg", lo, hi), 0.0, A.min, -2.0, A.mult)
+            folded.add(lo)
 
-        def esum(c, lo, hi):
-            flush()
-            mms(b("psE", lo, hi), [(sel(r), (T.ab[:, lo // 16:hi // 16, r, :], "ab", 16 * lo, 16 * hi)) for r in range(16)])
+        def judge_a(lo, hi):
+            gact(b("gx", 16 * lo, 16 * hi), XW, b(ACP, lo, hi), F.Copy)
 
-        def verdict(i, lo, hi):
+        def esum(lo, hi):
+            src = ["ab", "dg"] if lo in folded else ["ab"]
+            mms(b("psE", 256 + lo, 256 + hi), [(sel(r), four(x, lo, hi, r)) for x in src for r in range(16)])
+
+        def verdict(lo, hi):
             q0, q1 = lo // 16, hi // 16
-            tsc(b("okm", lo, hi), b("psE", lo, hi), b("tcol"), A.is_lt)
+            tsc(b("okm", lo, hi), b("psE", 256 + lo, 256 + hi), b("tcol"), A.is_lt)
             scan(b("cnt", lo, hi), b("rm", 0, hi - lo), b("okm", lo, hi), A.mult, A.add)
             tsc(b("t1", q0, q1), b("cnt", lo + 15, hi, 16), 6.5, A.is_lt, 2048.0 if last else 256.0, A.mult)
             tt(b("t2", q0, q1), b("t1", q0, q1), b(APL, q0, q1), A.add)
@@ -367,18 +403,31 @@ def rank_program(g, core, T, topo):
             else:
                 copy(b("off", q0, q1), b("t2", q0, q1))
 
+        def usum():
+            mms(b("psE", 0, 256), [(b("bo"), b("cw")), (b("bo"), b("zw"))])
+
+        def ucut():
+            act(b("hq"), b("psE", 0, 256), F.Identity, scale=1.0 / 4096, bias=192.0)
+            mms(b("psN", 0, 256), [(b("bo"), b("cw")), (b("bo"), b("zw")), (b("big"), b("hq"))])
+
+        def square():
+            act(b("uc"), b("psN", 0, 256), F.Identity, bias=192.0 * 4096)
+            mms(b("psP", 256, 512), [(b("odd2"), b("ones", 0, 256)), (b("odd"), b("zb")), (b("dk"), b("uc"))])
+            act(b("sq"), b("psN", 0, 256), F.Square, bias=192.0 * 4096)
+            act(b("sh"), b("sq"), F.Identity, scale=-1.0 / 32, bias=-16.5 / 32)
+
         def nextreq():
-            mms(b("psU", 256, 512), [(b("odd"), b("zb"))])
-            tsc(b("uu"), b("ui"), 4095, A.bitwise_and)
-            tt(b("sq"), b("uu"), b("uu"), A.mult)
-            tsc(b("sh"), b("sq"), 5, A.logical_shift_right)
-            tsc(b("psN", 0, 256), b("uu"), b("kcol"), A.mult)
-            tt(b("s1"), b("sh"), b("psN", 0, 256), A.add)
-            tt(b("s2"), b("s1"), b("psU", 256, 512), A.add)
+            tt(b("s2"), b("sh"), b("psP", 256, 512), A.add)
             if last:
                 tsc(b("cr"), b("s2"), 2047, A.bitwise_and)
-                copy(b("yco"), b("cr"))
-                dma("s", "o_yc", hbm(T.yc), b("yco"))
+
+        def small_out():
+            act(b("yco"), b("cr"), F.Identity, scale=-1.0, bias=2047.0)
+            dma("s", "o_yc", hbm(T.yc), b("yco"))
+
+        def z_out():
+            act(b("zo"), b("zb"), F.Identity, bias=-1280.0)
+            dma("s", "o_yz", hbm(T.yz), b("zo"))
 
         def arrive_x():
             if t == 0:
@@ -388,30 +437,34 @@ def rank_program(g, core, T, topo):
 
         def yo_own():
             for k in range(8):
-                act(b("yo", k, 2048, 8), b("xw", 512 * k, 512 * k + 256), F.Copy)
+                copy(b("yo", k, 2048, 8), b("xw", 512 * k, 512 * k + 256))
 
-        def final(i, lo, hi):
+        def final(lo, hi):
             put(b("yo", 8 * lo, 8 * hi + 2048), b("off", lo // 16, hi // 16), b(AV, lo, hi))
-            dma("s", "o_yx%d" % i, (T.yx[:, 8 * lo:8 * hi], None, 0, 0), b("yo", 8 * lo, 8 * hi))
+            dma("s", "o_yx%d" % lo, (T.yx[:, 8 * lo:8 * hi], None, 0, 0), b("yo", 8 * lo, 8 * hi))
 
-        BYCHUNK = {"n": names_v, "b": names_abs, "A": names_a, "r": least, "s": raised, "g": values, "h": extremes, "i": halved,
-                   "j": judge_v, "k": judge_abs, "J": judge_a, "e": esum, "K": lambda c, lo, hi: kspread(c)}
-        BYPART = {"p": places_sum, "q": places, "v": verdict, "E": final,
-                  "x": lambda i, lo, hi: put(XW, b("plu", lo // 16, hi // 16), b(VV, lo, hi)),
-                  "d": lambda i, lo, hi: put(DW, b("plu", lo // 16, hi // 16), b(CP, lo, hi)),
-                  "D": lambda i, lo, hi: put(DW, b("off", lo // 16, hi // 16), b(ACP, lo, hi))}
-        ONCE = {"X": arrive_x, "N": nextreq, "L": lambda: tail(b("s2")), "Y": yo_own, "Z": yz_out,
-                "P": lambda: send(t, APL, PL, "rp%d" % t, 0, 16)}
-        for tok in (SCHEDL if last else SCHED).split():
-            k, i = tok[0], int(tok[1:] or 0)
-            if k in BYCHUNK:
-                BYCHUNK[k](i, *CHUNKS[i])
-            elif k in BYPART:
-                BYPART[k](i, *PARTS[i])
+        RANGED = {"n": names_v, "b": names_abs, "A": names_a, "B": names_ps, "r": least, "R": raised, "g": values_v, "h": extremes_v,
+                  "G": values_a, "H": extremes_a, "O": risen, "z": weigh, "Z": weigh_v,
+                  "i": lambda lo, hi: halved(lo, hi, False), "I": lambda lo, hi: halved(lo, hi, True), "p": places_sum, "q": places, "j": spread_v, "w": judge_v,
+                  "m": judge_fold, "J": judge_a, "e": esum, "v": verdict, "E": final, "K": kspread,
+                  "1": lambda lo, hi: psub(lo, hi, "kt", "xh", "idh"), "2": lambda lo, hi: psub(lo, hi, "vt", "gx", "idb"),
+                  "a": lambda lo, hi: act(b(VV, lo, hi), b("psV", lo, hi), F.Abs),
+                  "k": lambda lo, hi: act(four("ab", lo, hi), ring(lo, hi), F.Abs),
+                  "o": lambda lo, hi: act(four("ab", lo, hi), four("dg", lo, hi), F.Abs),
+                  "c": lambda lo, hi: send(t, ACP, CP, "rc%d_%d" % (t, lo), lo, hi),
+                  "s": lambda lo, hi: send(t, AV, VV, "rs%d_%d" % (t, lo), lo, hi),
+                  "x": lambda lo, hi: put(XW, b("plu", lo // 16, hi // 16), b(VV, lo, hi)),
+                  "d": lambda lo, hi: put(DW, b("plu", lo // 16, hi // 16), b(CP, lo, hi)),
+                  "D": lambda lo, hi: put(DW, b("off", lo // 16, hi // 16), b(ACP, lo, hi))}
+        ONCE = {"X": arrive_x, "u": usum, "y": ucut, "S": square, "N": nextreq, "L": split, "l": keyed, "M": listed,
+                "Y": yo_own, "P": send_places, "C": small_out, "F": z_out, "W": later if t == 0 else lambda: None, "V": latest if t == 0 else lambda: None}
+        for k, lo, hi in tokens(SCHEDL if last else SCHED):
+            if k in RANGED:
+                RANGED[k](lo, hi)
             elif k == "U":
-                trans("kt", "k5", i, 0)
+                keys_t(lo)
             elif k == "T":
-                trans("vt", AV, i, 256)
+                trans("vt", b(AV, 128 * lo, 128 * lo + 128), lo, -1.0)
             else:
                 ONCE[k]()
     for s in sorted(count):

@@ -3,12 +3,13 @@ from concourse.mybir import AluOpType, ActivationFunctionType
 A = AluOpType
 F = ActivationFunctionType
 STEPS = 3
-READ = "X A02 102 A58 B02 n25 r02 R02 b25 168 156 A8a 18a Aad r25 g02 1ac B58 B8a 1cd Bad R25 h02 g25 r58 O58 r8a W Adg rad 1de I02 Oad O8a Gad 1eg g58 h25 h58 Bdg I25 a25 a02 Had rdg Iad I58 g8a Odg c05 Gdg z02 h8a z25 z58 cad I8a z8a a58 c5a a8a p0a aad Hdg zad idg Zdg V adg q0a x0a s05 u y pag qag s5a S sad sdg cdg xag P"
-SCHED = READ + " T0 J04 j8b J48 N 202 224 T1 k04 246 w8b jbe m8b 268 k48 wbe e8b Jeg e08 mbe 2eg L keg v08 ebe d0g eeg l K25 U1 U0 D08 v8g D8g M"
-SCHEDL = READ + " T0 J48 268 J04 246 T1 k48 202 224 k04 N j8b jbe wbe mbe ebe w8b F Y m8b C e08 Jeg 2eg v08 e8b E08 v8e E8e keg eeg veg Eeg"
-BIG = 8192.0
+READ = "/ 868 802 0 n25 8bc A58 A02 168 102 856 b25 156 B02 B58 X Abe r25 A8b r02 r58 Aeg W R02 R25 c05 % 1bc 88a O58 8ab 18a 1ab 8ce 8eg 1ce B8b 1eg Beg Bbe g02 g25 h02 h25 I05 r8b 405 g58 O8b c5b rbe G8b a05 s05 Obe 305 Gbe h58 reg Oeg cbg H8b Geg z05 Hbe V I5b 45b Heg 35b z5b #be #eg p0b a5b s5b Zbg u 50b 4bg fbg 60b y 70b abg sbg qbg P S T05 x0a xag"
+SCHED = READ + " J25 j58 J02 w58 924 902 202 945 224 245 m58 Jeg j8b k02 Tbg k25 w8b e58 N Jbe 9eg 2eg e05 L v08 9bc 2bc o8b keg 9ce 2ce kbe d0g e8b ebg D08 l v8g U0 D8g K25 U1 M"
+SCHEDL = READ + " Y 924 J25 j58 w58 945 902 245 224 J02 202 m58 j8b Jeg k25 Tbg e58 9eg 2eg k02 e05 9bc w8b N Jbe m8b keg v08 9ce 2bc 2ce E08 e8b kbe F C ebg v8g E8g"
+BIG = 131072.0
 ROUND = 12582912.0
 ROUND4096 = ROUND * 4096
+YG = 8
 WID = 1024
 
 
@@ -22,10 +23,10 @@ SCRATCH = {"psS": ("psum", [128, 2048], "float32"), "psV": ("psum", [128, 512], 
            "ab": ("sbuf", [128, 16, 256], "bfloat16"), "dg": ("sbuf", [128, 16, 256], "bfloat16")}
 for _d, _w, _names in (
         ("int32", 4096, "dw"), ("bfloat16", 4096, "xw yo"), ("int32", 2048, "reci ra rb"), ("float16", 2048, "xt"),
-        ("int32", 1, "muli thi"), ("float32", 1, "kcol tcol ocol ocol2"), ("int32", 16, "p8 pa pb pc pi p9"),
-        ("int32", 256, "reqi ni ki sh s2 cr"), ("bfloat16", 256, "aimb wtb cw nk nib mm mid hq kt vt zc zo okm cnt offc"),
-        ("float32", 256, "sq yco"), ("float16", 256, "zw zb aimc uc"), ("uint16", 256, "cl"),
-        ("bfloat16", 128, "bt bo idb nidb big mhalf odd odd2"), ("float16", 128, "idh hid dk"), ("bfloat16", 1024, "ones"),
+        ("int32", 1, "muli thi"), ("float32", 1, "kcol tcol ocol ocol2 rcol"), ("int32", 16, "p8 pa pb pc pi p9"),
+        ("int32", 256, "reqi ni ki sh s2 cr"), ("bfloat16", 256, "aimb wtb cw nk nib mm mid hq kt zc zo okm cnt offc irow"),
+        ("float32", 256, "sq yco ud"), ("float16", 256, "zw zb zs aimc uc"), ("uint16", 256, "cl"),
+        ("bfloat16", 128, "bt bo idb nidb big mhalf odd odd2 tiny colr offd"), ("float16", 128, "idh hid dk"), ("bfloat16", 1024, "ones vt"),
         ("bfloat16", 2048, "en sel"), ("bfloat16", WID, "nb rm xoff"), ("bfloat16", 16, "ic"), ("float32", 16, "t1 t2 ic8"),
         ("uint16", 16, "plu off"), ("bfloat16", 4096, "kz kb vz vb gx yb sc"), ("float16", 4096, "xh xb xg mxa mna"),
         ("float16", 2048, "mx mn")):
@@ -155,9 +156,9 @@ def rank_program(g, core, T, topo):
     def iota(o, pat, base, cm):
         op("g", [lambda: g.iota(o[0], pat, base, cm, allow_small_or_imprecise_dtypes=True)], [o], [])
 
-    def mms(o, terms):
+    def mms(o, terms, start=True, stop=True):
         k = len(terms) - 1
-        op("p", [lambda j=j, l=l, r=r: P.matmul(o[0], l[0], r[0], j == 0, j == k) for j, (l, r) in enumerate(terms)],
+        op("p", [lambda j=j, l=l, r=r: P.matmul(o[0], l[0], r[0], start and j == 0, stop and j == k) for j, (l, r) in enumerate(terms)],
            [o], [x for t in terms for x in t], terms)
 
     def sel(r): return b("sel", 128 * r, 128 * r + 128)
@@ -184,36 +185,46 @@ def rank_program(g, core, T, topo):
     LW = 2048 // LOADS
     for h in range(LOADS):
         dma("s", "l_rec%d" % h, b("reci", LW * h, LW * h + LW), (T.rec[:, LW * h:LW * h + LW], None, 0, 0))
-    dma("s", "l_mul", b("muli"), hbm(T.mul))
-    dma("s", "l_th", b("thi"), hbm(T.th))
     dma("s", "l_aim", b("aimb"), hbm(T.aim))
     dma("s", "l_wt", b("wtb"), hbm(T.wt))
+    dma("s", "l_mul", b("muli"), hbm(T.mul))
+    dma("s", "l_th", b("thi"), hbm(T.th))
 
     fill(b("ones"), 1.0)
+    fill((T.offc[64:128, :], "offc", 0, 256), -1.0 / 256)
     o128 = b("ones", 0, 128)
     iota(b("p8"), [[0, 16]], 0, 1)
     iota(b("pb"), [[16, 16]], 0, 0)
     affine(b("idb"), o128, [[-1, 128]], A.is_equal, 0, 1)
+    iota(b("colr"), [[0, 8], [1, 16]], 0, 0)
     affine(b("en", 0, 1024), b("ones", 0, 1024), [[-1, 64], [0, 16]], A.is_equal, 0, 1)
     affine(b("en", 1024, 2048), b("ones", 0, 1024), [[-1, 64], [0, 16]], A.is_equal, -64, 1)
     iota(b("xoff"), [[0, WID // 256], [256, 16], [0, 16]], -2048, 0)
     iota((T.offc[0:64, :], "offc", 0, 256), [[0, 16], [-4, 16]], 32, 0)
+    iota(b("irow"), [[1, 256]], 0, 0)
     affine(b("bt"), o128, [[-16, 8], [0, 16]], A.is_ge, 0, 1)
     affine(b("bo"), b("bt"), [[16, 8], [0, 16]], A.is_ge, 15, -1)
-    for r in range(16):
-        affine(sel(r), b("bo"), [[0, 8], [1, 16]], A.is_equal, -r, 0)
+
+    def selectors():
+        for r in range(16):
+            affine(sel(r), b("bo"), [[0, 8], [1, 16]], A.is_equal, -r, 0)
     fill(b("rm"), 1.0)
     fill(b("rm", 0, WID, 16), 0.0)
-    fill(b("nb"), 0.0)
-    fill(b("nb", 0, WID, 16), BIG)
     fill(b("mhalf"), -0.5)
-    for x, lo, hi in tokens(SCHED):
-        if x == "K":
-            fill(b("kz", 16 * lo, 16 * hi), 0.0)
+    fill(b("tiny"), 1.0 / 65536)
     tsc(b("pa"), b("p8"), 15, A.bitwise_and)
     tt(b("pc"), b("pa"), b("pb"), A.add)
-    act(b("idh"), b("idb"), F.Copy)
+    tsc(b("ic"), b("pc"), 1.0 / 512, A.mult)
+    tsc(b("ic8"), b("pc"), 8.0, A.mult)
+    copy(b("rcol"), b("pa", 0, 1))
+    tsc(b("ocol"), b("pa", 0, 1), -2.0, A.mult, -1.0, A.add)
+    tsc(b("ocol2"), b("pa", 0, 1), 2560.0, A.mult, 1280.0, A.add)
+    for x, lo, hi in tokens(SCHED):
+        if x == "K":
+            act(b("kz", 16 * lo, 16 * hi), b("ones", 0, 16 * (hi - lo)), F.Copy, scale=0.0)
     act(b("nidb"), b("idb"), F.Copy, scale=-1.0)
+    act(b("idh"), b("idb"), F.Copy)
+    act(b("nb"), b("rm"), F.Identity, scale=-BIG, bias=BIG)
 
     def split(src="s2"):
         tsc(b("ki"), b(src), 7, A.bitwise_and)
@@ -227,23 +238,37 @@ def rank_program(g, core, T, topo):
     def listed():
         act(b("cl"), b("psN", 0, 256), F.Identity, bias=1791.0)
 
-    def kspread(lo, hi):
-        copy(b("kz", 16 * lo, 16 * hi, 16), b("nk", lo, hi))
+    def kspread(lo, hi, first=False):
+        if first or ("+", lo, hi) not in tokens(SCHED):
+            copy(b("kz", 16 * lo, 16 * hi, 16), b("nk", lo, hi))
         scan(b("kb", 16 * lo, 16 * hi), b("rm", 0, 16 * (hi - lo)), b("kz", 16 * lo, 16 * hi), A.mult, A.add)
 
-    def trans(dst, src, h, scale):
-        k = 256 + 128 * h
-        mms(b("psV", k, k + 128), [(src, b("idb"))])
-        act(b(dst, 128 * h, 128 * h + 128), b("psV", k, k + 128), F.Copy, scale=scale)
+    turned = {"kt": [], "vt": []}
 
-    def keys_t(h): trans("kt", b("nk", 128 * h, 128 * h + 128), h, 1.0)
+    def rows(name, n, lo, hi): return (T[name][0:n, lo:hi], name, lo, hi)
+
+    def trans(dst, src, lo, hi, scale):
+        if (lo, hi) not in turned[dst]:
+            turned[dst].append((lo, hi))
+        k = 128 * turned[dst].index((lo, hi))
+        p = rows("psV", hi - lo, 256 + k % 256, 384 + k % 256)
+        mms(p, [(b(src, lo, hi), b("idb"))])
+        act(rows(dst, hi - lo, k, k + 128), p, F.Copy, scale=scale)
+
+    def keys_t(h): trans("kt", "nk", 128 * h, 128 * h + 128, 1.0)
     def ring(lo, hi): return b("psS", 16 * lo % 2048, 16 * lo % 2048 + 16 * (hi - lo))
 
-    def psub(lo, hi, tname, data, ident):
-        cuts = [lo] + [m for m in range(0, 256, 32) if lo < m < hi] + [hi]
-        for m, e in zip(cuts, cuts[1:]):
-            h, k = 128 * (m // 128), 16 * (m % 128)
-            mms(ring(m, e), [(b(tname, h, h + 128), b("en", k, k + 16 * (e - m))), (b(ident), b(data, 16 * m, 16 * e))])
+    def pspread(lo, hi, tname, now):
+        h, (l, e) = [(j, x) for j, x in enumerate(turned[tname]) if x in now and x[0] <= lo and hi <= x[1]][0]
+        k = 16 * (lo - l)
+        mms(bank(lo, hi), [(rows(tname, e - l, 128 * h, 128 * h + 128), rows("en", e - l, k, k + 16 * (hi - lo)))], stop=False)
+
+    def padd(lo, hi, data, ident):
+        mms(bank(lo, hi), [(b(ident), b(data, 16 * lo, 16 * hi))], start=False)
+
+    def bank(lo, hi):
+        p = ring(lo, hi)
+        return (p[0], p[1], p[2] // 512 * 512, p[2] // 512 * 512 + 512)
 
     def low(h): tsc(b("ra", LW * h, LW * h + LW), b("reci", LW * h, LW * h + LW), 2047, A.bitwise_and)
     def wide(h): act(b("rb", LW * h, LW * h + LW), b("ra", LW * h, LW * h + LW), F.Identity, scale=512.125, bias=-0.4375)
@@ -251,27 +276,23 @@ def rank_program(g, core, T, topo):
     def high(h):
         act(b("xt", LW * h, LW * h + LW), b("reci", LW * h, LW * h + LW), F.Identity, bias=1279.5 + 1.0 / 4096, scale=1.0 / 2048)
 
-    def names(h):
+    def names(lo, hi):
         for k in range(8):
-            c = 512 * k + 128 * h
-            tsc(b("dw", c, c + 128), b("rb", 1024 * h + k, 1024 * h + 1024, 8), 3839, A.bitwise_and)
+            tsc(b("dw", 512 * k + lo // 8, 512 * k + hi // 8), b("rb", lo + k, hi, 8), 3839, A.bitwise_and)
     split("reqi")
     keyed(True)
     low(0), wide(0), listed()
-    tsc(b("ic"), b("pc"), 1.0 / 512, A.mult)
-    tsc(b("ic8"), b("pc"), 8.0, A.mult)
-    tsc(b("ocol"), b("pa", 0, 1), -2.0, A.mult, -1.0, A.add)
-    tsc(b("ocol2"), b("pa", 0, 1), 2560.0, A.mult, 1280.0, A.add)
+    tsc(b("offd"), b("colr"), b("rcol"), A.not_equal, 2 * BIG, A.mult)
     low(1), wide(1), keys_t(0), keys_t(1), high(0)
     for x, lo, hi in tokens(SCHED):
         if x == "K":
-            kspread(lo, hi)
-    low(2), wide(2), high(1), names(0), low(3), wide(3), high(2), high(3)
-    tsc(b("kcol"), b("muli"), -1.0, A.mult, 1920.0, A.add)
-    copy(b("tcol"), b("thi"))
-    fill((T.offc[64:128, :], "offc", 0, 256), -1.0 / 256)
-    names(1)
-    act(b("hid"), b("idb"), F.Copy, scale=0.5)
+            kspread(lo, hi, True)
+    low(2), wide(2), high(1), names(0, 2 * LW), low(3), wide(3), high(2)
+    names(2 * LW, 4 * LW)
+
+    def soon():
+        high(3)
+        act(b("hid"), b("idb"), F.Copy, scale=0.5)
 
     def late():
         for k in range(8):
@@ -284,18 +305,24 @@ def rank_program(g, core, T, topo):
     def latest():
         act(b("cw"), b("wtb"), F.Identity, scale=128.0, bias=-128.0)
         act(b("big"), b("idb"), F.Copy, scale=-4096.0)
+        act(b("kcol"), b("muli"), F.Identity, scale=-1.0, bias=1920.0)
+        act(b("tcol"), b("thi"), F.Copy)
         act(b("dk"), b("idb"), F.Copy, scale=b("kcol"))
         act(b("odd"), b("idb"), F.Copy, scale=b("ocol"))
         act(b("odd2"), b("idb"), F.Copy, scale=b("ocol2"))
+
+    def zeros():
         spread = [k for k in tokens(SCHED + " " + SCHEDL) if k[0] == "j"]
         lo, hi = min(k[1] for k in spread), max(k[2] for k in spread)
         iota(b("vz", 16 * lo, 16 * hi), [[0, 16 * (hi - lo)]], 0, 0)
+
+    def now(last): return tokens(SCHEDL if last else SCHED)
 
     DW, XW = b("dw"), b("xw")
     for t in range(STEPS):
         last = t == STEPS - 1
         CP, VV, PL, ACP, AV, APL = "cp%d" % t, "vv%d" % t, "pl%d" % t, "acp%d" % t, "av%d" % t, "apl%d" % t
-        folded, toks = set(), set(tokens(READ))
+        folded, toks = set(), set(now(last))
 
         def names_v(lo, hi):
             gtt(b("xb", 16 * lo, 16 * hi), DW, b("cl", lo, hi), b("kb", 16 * lo, 16 * hi), A.add)
@@ -311,12 +338,18 @@ def rank_program(g, core, T, topo):
 
         def least(lo, hi):
             scan(b("sc", 16 * lo, 16 * hi), b("nb", 0, 16 * (hi - lo)), b("yb", 16 * lo, 16 * hi), A.max, A.min)
+            if ("Q", lo, hi) in toks:
+                return mms(b("psN", 256 + lo, 256 + hi), [(b("idb"), b("nib", lo, hi)), (b("nidb"), b("sc", 16 * lo + 15, 16 * hi, 16))])
             tt(b("mm", lo, hi), b("sc", 16 * lo + 15, 16 * hi, 16), b("nib", lo, hi), A.min)
             o = b("psP", 256 + lo, 256 + hi) if ("R", lo, hi) in toks else b("psN", lo, hi)
             mms(o, [(b("nidb"), b("nk", lo, hi)), (b("nidb"), b("mm", lo, hi))])
 
         def raised(lo, hi):
             tsc(b(CP, lo, hi), b("psP", 256 + lo, 256 + hi), 1791.0, A.add)
+
+        def rise(lo, hi):
+            act(b("mm", lo, hi), b("psN", 256 + lo, 256 + hi), F.Relu)
+            mms(b("psN", lo, hi), [(b("nidb"), b("nk", lo, hi)), (b("nidb"), b("nib", lo, hi)), (b("idb"), b("mm", lo, hi))])
 
         def risen(lo, hi):
             act(b(CP, lo, hi), b("psN", lo, hi), F.Identity, bias=1791.0)
@@ -339,15 +372,24 @@ def rank_program(g, core, T, topo):
             w, e = (16 * lo, 16 * hi), (16 * lo + 15, 16 * hi, 16)
             scan(b("mxa", *w), b("rm", 0, 16 * (hi - lo)), b("xg", *w), A.mult, A.max)
             scan(b("mna", *w), b("nb", 0, 16 * (hi - lo)), b("xg", *w), A.max, A.min)
-            mms(b("psE", lo, hi), [(b("hid"), b("mhalf", 0, hi - lo)), (b("hid"), b("mxa", *e)), (b("hid"), b("mna", *e))])
+            if ("#", lo, hi) not in toks:
+                mms(b("psE", lo, hi), [(b("hid"), b("mhalf", 0, hi - lo)), (b("hid"), b("mxa", *e)), (b("hid"), b("mna", *e))])
+
+        def halved_v(lo, hi):
+            e = (16 * lo + 15, 16 * hi, 16)
+            tt(b("zs", lo, hi), b("mxa", *e), b("mna", *e), A.add)
+            tsc(b("zb", lo, hi), b("zs", lo, hi), 0.5, A.mult, 1279.75, A.add)
 
         def halved(lo, hi, scalar):
             if scalar:
                 act(b("zb", lo, hi), b("psE", lo, hi), F.Identity, bias=1280.0)
             else:
                 tsc(b("zb", lo, hi), b("psE", lo, hi), 1280.0, A.add)
-            if ("z", lo, hi) in toks:
-                mms(b("psP", 256 + lo, 256 + hi), [(b("idb"), b("mid", lo, hi)), (b("idh"), b("zb", lo, hi))])
+
+        def less_mid(lo, hi):
+            mms(b("psP", 256 + lo, 256 + hi), [(b("idb"), b("mid", lo, hi)), (b("idh"), b("zb", lo, hi))])
+
+        def less_aim(lo, hi):
             mms(b("psV", lo, hi), [(b("idh"), b("aimc", lo, hi)), (b("idh"), b("zb", lo, hi))])
 
         def weigh(lo, hi):
@@ -361,11 +403,27 @@ def rank_program(g, core, T, topo):
             q0, q1 = lo // 16, hi // 16
             mms(b("psP", q0, q1), [(b("idb"), b("ic", q0, q1))] + [(sel(r), b("zw", lo + r, hi, 16)) for r in range(16)])
 
+        def places_wide(lo, hi):
+            mms(b("psP", 256 + lo, 256 + hi), [(b("tiny"), b("irow", lo, hi)), (b("idb"), b("offd", 0, hi - lo)), (b("bo"), b("zw", lo, hi))])
+
         def places(lo, hi):
             q0, q1 = lo // 16, hi // 16
-            tsc(b("pi", q0, q1), b("psP", q0, q1), 512.0, A.mult)
+            if ("f", lo, hi) in toks:
+                scan(b("ud", lo, hi), b("nb", 0, hi - lo), b("psP", 256 + lo, 256 + hi), A.add, A.min)
+                tsc(b("pi", q0, q1), b("ud", lo + 15, hi, 16), 512.0, A.mult)
+            else:
+                tsc(b("pi", q0, q1), b("psP", q0, q1), 512.0, A.mult)
             tsc(b("p9" if last else PL, q0, q1), b("pi", q0, q1), 3839, A.bitwise_and)
             copy(b("plu", q0, q1), b("p9" if last else PL, q0, q1))
+
+        def pick(lo, hi): scan(b("ud", lo, hi), b("nb", 0, hi - lo), b("psP", 256 + lo, 256 + hi), A.add, A.min)
+
+        def place_a(lo, hi):
+            src = b("ud", lo + 15, hi, 16) if ("f", lo, hi) in toks else b("psP", lo // 16, hi // 16)
+            act(b("pi", lo // 16, hi // 16), src, F.Identity, scale=512.0)
+
+        def place_b(lo, hi): tsc(b("p9" if last else PL, lo // 16, hi // 16), b("pi", lo // 16, hi // 16), 3839, A.bitwise_and)
+        def place_c(lo, hi): act(b("plu", lo // 16, hi // 16), b("p9" if last else PL, lo // 16, hi // 16), F.Copy)
 
         def send_places():
             if last:
@@ -374,7 +432,8 @@ def rank_program(g, core, T, topo):
             send(t, APL, PL, "rp%d" % t, 0, 16)
 
         def spread_v(lo, hi):
-            copy(b("vz", 16 * lo, 16 * hi, 16), b(AV, lo, hi))
+            if not [k for k in toks if k[0] == "t" and k[1] <= lo and hi <= k[2]]:
+                copy(b("vz", 16 * lo, 16 * hi, 16), b(AV, lo, hi))
             scan(b("vb", 16 * lo, 16 * hi), b("rm", 0, 16 * (hi - lo)), b("vz", 16 * lo, 16 * hi), A.mult, A.add)
 
         def judge_v(lo, hi):
@@ -398,10 +457,11 @@ def rank_program(g, core, T, topo):
             scan(b("cnt", lo, hi), b("rm", 0, hi - lo), b("okm", lo, hi), A.mult, A.add)
             tsc(b("t1", q0, q1), b("cnt", lo + 15, hi, 16), 6.5, A.is_lt, 2048.0 if last else 256.0, A.mult)
             tt(b("t2", q0, q1), b("t1", q0, q1), b(APL, q0, q1), A.add)
-            if last:
-                tsc(b("off", q0, q1), b("t2", q0, q1), -8.0 * lo, A.add)
-            else:
-                copy(b("off", q0, q1), b("t2", q0, q1))
+            if ("*", lo, hi) not in toks:
+                tsc(b("off", q0, q1), b("t2", q0, q1), -8.0 * lo if last else 0.0, A.add)
+
+        def offsets(lo, hi):
+            act(b("off", lo // 16, hi // 16), b("t2", lo // 16, hi // 16), F.Identity, bias=-8.0 * lo if last else 0.0)
 
         def usum():
             mms(b("psE", 0, 256), [(b("bo"), b("cw")), (b("bo"), b("zw"))])
@@ -437,17 +497,25 @@ def rank_program(g, core, T, topo):
 
         def yo_own():
             for k in range(8):
-                copy(b("yo", k, 2048, 8), b("xw", 512 * k, 512 * k + 256))
+                if k < YG:
+                    affine(b("yo", k, 2048, 8), b("xw", 512 * k, 512 * k + 256), [[0, 256]], A.is_ge, 0, 0)
+                else:
+                    copy(b("yo", k, 2048, 8), b("xw", 512 * k, 512 * k + 256))
 
         def final(lo, hi):
             put(b("yo", 8 * lo, 8 * hi + 2048), b("off", lo // 16, hi // 16), b(AV, lo, hi))
             dma("s", "o_yx%d" % lo, (T.yx[:, 8 * lo:8 * hi], None, 0, 0), b("yo", 8 * lo, 8 * hi))
 
         RANGED = {"n": names_v, "b": names_abs, "A": names_a, "B": names_ps, "r": least, "R": raised, "g": values_v, "h": extremes_v,
-                  "G": values_a, "H": extremes_a, "O": risen, "z": weigh, "Z": weigh_v,
+                  "G": values_a, "H": extremes_a, "O": risen, "Q": rise, "<": pick, "#": halved_v, "*": offsets,
+                  "t": lambda lo, hi: act(b("vz", 16 * lo, 16 * hi, 16), b(AV, lo, hi), F.Copy),
+                  "+": lambda lo, hi: act(b("kz", 16 * lo, 16 * hi, 16), b("nk", lo, hi), F.Copy), "5": place_a, "6": place_b, "7": place_c, "z": weigh, "Z": weigh_v, "3": less_mid, "4": less_aim, "f": places_wide,
                   "i": lambda lo, hi: halved(lo, hi, False), "I": lambda lo, hi: halved(lo, hi, True), "p": places_sum, "q": places, "j": spread_v, "w": judge_v,
                   "m": judge_fold, "J": judge_a, "e": esum, "v": verdict, "E": final, "K": kspread,
-                  "1": lambda lo, hi: psub(lo, hi, "kt", "xh", "idh"), "2": lambda lo, hi: psub(lo, hi, "vt", "gx", "idb"),
+                  "8": lambda lo, hi: pspread(lo, hi, "kt", [(0, 128), (128, 256)]), "1": lambda lo, hi: padd(lo, hi, "xh", "idh"),
+                  "T": lambda lo, hi: trans("vt", AV, lo, hi, -1.0),
+                  "9": lambda lo, hi: pspread(lo, hi, "vt", [k[1:] for k in tokens(SCHEDL if last else SCHED) if k[0] == "T"]),
+                  "2": lambda lo, hi: padd(lo, hi, "gx", "idb"),
                   "a": lambda lo, hi: act(b(VV, lo, hi), b("psV", lo, hi), F.Abs),
                   "k": lambda lo, hi: act(four("ab", lo, hi), ring(lo, hi), F.Abs),
                   "o": lambda lo, hi: act(four("ab", lo, hi), four("dg", lo, hi), F.Abs),
@@ -457,14 +525,14 @@ def rank_program(g, core, T, topo):
                   "d": lambda lo, hi: put(DW, b("plu", lo // 16, hi // 16), b(CP, lo, hi)),
                   "D": lambda lo, hi: put(DW, b("off", lo // 16, hi // 16), b(ACP, lo, hi))}
         ONCE = {"X": arrive_x, "u": usum, "y": ucut, "S": square, "N": nextreq, "L": split, "l": keyed, "M": listed,
-                "Y": yo_own, "P": send_places, "C": small_out, "F": z_out, "W": later if t == 0 else lambda: None, "V": latest if t == 0 else lambda: None}
+                "Y": yo_own, "P": send_places, "C": small_out, "F": z_out, "W": later if t == 0 else lambda: None,
+                "0": soon if t == 0 else lambda: None, "/": selectors if t == 0 else lambda: None,
+                "%": zeros if t == 0 else lambda: None, "V": latest if t == 0 else lambda: None}
         for k, lo, hi in tokens(SCHEDL if last else SCHED):
             if k in RANGED:
                 RANGED[k](lo, hi)
             elif k == "U":
                 keys_t(lo)
-            elif k == "T":
-                trans("vt", b(AV, 128 * lo, 128 * lo + 128), lo, -1.0)
             else:
                 ONCE[k]()
     for s in sorted(count):

from concourse.mybir import AluOpType, ActivationFunctionType

A = AluOpType
F = ActivationFunctionType
STEPS = 3
READ = "/ 868 802 0 n25 8bc A58 A02 168 102 856 b25 156 B02 B58 X Abe r25 A8b r02 r58 Aeg W R02 R25 c05 % 1bc 88a O58 8ab 18a 1ab 8ce 8eg 1ce B8b 1eg Beg Bbe g02 g25 h02 h25 I05 r8b 405 g58 O8b c5b rbe G8b a05 s05 Obe 305 Gbe h58 reg Oeg cbg H8b Geg z05 Hbe V I5b 45b Heg 35b z5b #be #eg p0b a5b s5b Zbg u 50b 4bg fbg 60b y 70b abg sbg qbg P S T05 x0a xag"
SCHED = READ + " J25 j58 J02 w58 924 902 202 945 224 245 m58 Jeg j8b k02 Tbg k25 w8b e58 N Jbe 9eg 2eg e05 L v08 9bc 2bc o8b keg 9ce 2ce kbe d0g e8b ebg D08 l v8g U0 D8g K25 U1 M"
SCHEDL = READ + " Y 924 J25 j58 w58 945 902 245 224 J02 202 m58 j8b Jeg k25 Tbg e58 9eg 2eg k02 e05 9bc w8b N Jbe m8b keg v08 9ce 2bc 2ce E08 e8b kbe F C ebg v8g E8g"
BIG = 131072.0
ROUND = 12582912.0
ROUND4096 = ROUND * 4096
YG = 8
WID = 1024


def tokens(s):
    return [(k[0], 16 * int(k[1], 17), 16 * int(k[2], 17)) if len(k) == 3 else (k[0], int(k[1:] or 0), 0) for k in s.split()]


SENDS = [k for k in tokens(READ) if k[0] in "cs"]
SCRATCH = {"psS": ("psum", [128, 2048], "float32"), "psV": ("psum", [128, 512], "float32"), "psE": ("psum", [128, 512], "float32"),
           "psP": ("psum", [128, 512], "float32"), "psN": ("psum", [128, 512], "float32"),
           "ab": ("sbuf", [128, 16, 256], "bfloat16"), "dg": ("sbuf", [128, 16, 256], "bfloat16")}
for _d, _w, _names in (
        ("int32", 4096, "dw"), ("bfloat16", 4096, "xw yo"), ("int32", 2048, "reci ra rb"), ("float16", 2048, "xt"),
        ("int32", 1, "muli thi"), ("float32", 1, "kcol tcol ocol ocol2 rcol"), ("int32", 16, "p8 pa pb pc pi p9"),
        ("int32", 256, "reqi ni ki sh s2 cr"), ("bfloat16", 256, "aimb wtb cw nk nib mm mid hq kt zc zo okm cnt offc irow"),
        ("float32", 256, "sq yco ud"), ("float16", 256, "zw zb zs aimc uc"), ("uint16", 256, "cl"),
        ("bfloat16", 128, "bt bo idb nidb big mhalf odd odd2 tiny colr offd"), ("float16", 128, "idh hid dk"), ("bfloat16", 1024, "ones vt"),
        ("bfloat16", 2048, "en sel"), ("bfloat16", WID, "nb rm xoff"), ("bfloat16", 16, "ic"), ("float32", 16, "t1 t2 ic8"),
        ("uint16", 16, "plu off"), ("bfloat16", 4096, "kz kb vz vb gx yb sc"), ("float16", 4096, "xh xb xg mxa mna"),
        ("float16", 2048, "mx mn")):
    for _n in _names.split():
        SCRATCH[_n] = ("sbuf", [128, _w], _d)
for _t in range(STEPS):
    for _n, _w, _d in (("cp", 256, "uint16"), ("vv", 256, "bfloat16"), ("pl", 16, "int32")):
        SCRATCH["%s%d" % (_n, _t)] = SCRATCH["a%s%d" % (_n.replace("vv", "v"), _t)] = ("sbuf", [128, _w], _d)
LOADS = 4
SEMAPHORES = ["sv", "sa", "sp", "sg", "ls", "l_req", "l_aim", "l_wt", "l_mul", "l_th", "o_yc", "o_yz"]
SEMAPHORES += ["l_rec%d" % _h for _h in range(LOADS)] + ["o_yx%d" % _k[1] for _k in tokens(SCHEDL) if _k[0] == "E"]
for _t in range(STEPS):
    SEMAPHORES += ["rp%d" % _t] + ["r%s%d_%d" % (_k[0], _t, _k[1]) for _k in SENDS]


def tracker(g, T):
    Q = {"v": g.vector, "a": g.scalar, "p": g.tensor, "g": g, "s": g.sync}
    SEM = {"v": "sv", "a": "sa", "p": "sp", "g": "sg"}
    count, hist, snap = {}, {}, {}
    known = {q: {} for q in Q}

    def need(q, outs, ins):
        req = {}
        for lst, isw in ((ins, False), (outs, True)):
            for (_, name, lo, hi) in lst:
                ps = name[:2] == "ps"
                for (l2, h2, q2, src, n, w2) in hist.get(name, ()):
                    over = lo < h2 and l2 < hi
                    if q2 == q:
                        hit = over and w2
                    elif ps:
                        hit = lo // 512 <= (h2 - 1) // 512 and l2 // 512 <= (hi - 1) // 512
                    else:
                        hit = over and (isw or w2)
                    if hit:
                        req[src] = max(req.get(src, 0), n)
        k = known[q]
        for src in sorted(req, key=lambda s: -req[s]):
            n = req[src]
            if k.get(src, 0) >= n:
                continue
            Q[q].wait_ge(T.sem[src], n)
            k[src] = n
            for s2, n2 in snap.get((src, n), {}).items():
                if k.get(s2, 0) < n2:
                    k[s2] = n2

    def note(q, src, n, outs, ins, kq=None):
        snap[(src, n)] = dict(known.get(kq or q, {}))
        for lst, isw in ((ins, False), (outs, True)):
            for (_, name, lo, hi) in lst:
                h = hist.setdefault(name, [])
                h[:] = [e for e in h if not (e[0] == lo and e[1] == hi and e[2] == q and e[5] == isw)]
                h.append((lo, hi, q, src, n, isw))

    def op(q, calls, outs, ins, each=None):
        need(q, outs, [] if each else ins)
        for j, c in enumerate(calls):
            if each:
                need(q, [], each[j])
            i = c()
        s = SEM[q]
        i.then_inc(T.sem[s], 1)
        count[s] = count.get(s, 0) + 1
        note(q, s, count[s], outs, ins)

    def dma(q, sem, out, in_):
        o, i = [out] if out[1] else [], [in_] if in_[1] else []
        need(q, o, i)
        Q[q].dma_start(out[0], in_[0]).then_inc(T.sem[sem], 16)
        count[sem] = 16
        note("dma", sem, 16, o, i, q)

    return op, dma, need, note, count


def rank_program(g, core, T, topo):
    rank = T.rank_of(core)
    if rank is None:
        return
    op, dma, need, note, count = tracker(g, T)
    V, S, P = g.vector, g.scalar, g.tensor
    N = len(T.cores)

    def b(name, lo=0, hi=None, st=1):
        w = T[name].shape[1]
        hi = w if hi is None else hi
        if lo == 0 and hi == w and st == 1:
            return (T[name][:], name, lo, hi)
        return (T[name][:, lo:hi:st] if st > 1 else T[name][:, lo:hi], name, lo, hi)

    def back(name, lo, hi, st=1):
        return (T[name][:, hi - 1:(lo - 1 if lo else None):-st], name, lo, hi)

    def four(name, lo, hi, r=None):
        t = T[name]
        return (t[:, lo // 16:hi // 16, :] if r is None else t[:, lo // 16:hi // 16, 16 * r:16 * r + 16], name, 16 * lo, 16 * hi)

    def hbm(t): return (t[:], None, 0, 0)
    def ind(win, off): return T[win[1]][:, win[2]:win[3]].indirect(off[0])
    def copy(o, i): op("v", [lambda: V.tensor_copy(o[0], i[0])], [o], [i])
    def tt(o, x, y, f): op("v", [lambda: V.tensor_tensor(o[0], x[0], y[0], f)], [o], [x, y])

    def tsc(o, x, a, f, a2=None, f2=None):
        ins = [x] + ([a] if isinstance(a, tuple) else [])
        va = a[0] if isinstance(a, tuple) else a
        if f2 is None:
            op("v", [lambda: V.tensor_scalar(o[0], x[0], va, None, f)], [o], ins)
        else:
            op("v", [lambda: V.tensor_scalar(o[0], x[0], va, a2, f, f2)], [o], ins)

    def fill(o, c): op("v", [lambda: V.memset(o[0], c)], [o], [])
    def scan(o, d0, d1, f0, f1, first=0.0): op("v", [lambda: V.tensor_tensor_scan(o[0], d0[0], d1[0], first, f0, f1)], [o], [d0, d1])

    def act(o, i, f, bias=0.0, scale=1.0):
        col = [scale] if isinstance(scale, tuple) else []
        sc = scale[0] if col else scale
        op("a", [lambda: S.activation(o[0], i[0], f, bias=bias, scale=sc)], [o], [i] + col)

    def gact(o, win, off, f, bias=0.0, scale=1.0):
        op("a", [lambda: S.activation(o[0], ind(win, off), f, bias=bias, scale=scale)], [o], [win, off])

    def gtt(o, win, off, y, f): op("v", [lambda: V.tensor_tensor(o[0], ind(win, off), y[0], f)], [o], [win, off, y])
    def put(win, off, val): op("v", [lambda: V.tensor_copy(ind(win, off), val[0])], [win], [off, val])
    def affine(o, i, pat, f, base, cm): op("g", [lambda: g.affine_select(o[0], i[0], pat, f, 0.0, base, cm)], [o], [i])

    def iota(o, pat, base, cm):
        op("g", [lambda: g.iota(o[0], pat, base, cm, allow_small_or_imprecise_dtypes=True)], [o], [])

    def mms(o, terms, start=True, stop=True):
        k = len(terms) - 1
        op("p", [lambda j=j, l=l, r=r: P.matmul(o[0], l[0], r[0], start and j == 0, stop and j == k) for j, (l, r) in enumerate(terms)],
           [o], [x for t in terms for x in t], terms)

    def sel(r): return b("sel", 128 * r, 128 * r + 128)

    def eng(src, dst): return topo.engines(src, dst)[:8]
    for t in range(STEPS):
        n = len(eng(T.cores[(rank - 1 - t) % N], core))
        for x, lo, hi in SENDS:
            note("r", "r%s%d_%d" % (x, t, lo), n, [b(("acp%d" if x == "c" else "av%d") % t, lo, hi)], [])
            count["r%s%d_%d" % (x, t, lo)] = n
        note("r", "rp%d" % t, n, [b("apl%d" % t)], [])
        count["rp%d" % t] = n
    count["ls"] = 0

    def send(t, dname, sname, sem, lo, hi):
        dst = T.cores[(rank + 1 + t) % N]
        es = eng(core, dst)
        need("g", [], [b(sname, lo, hi)])
        ad = topo.addr(dst)
        g.remote_dma(b(dname, lo, hi)[0], b(sname, lo, hi)[0], T.sem[sem], T.sem.ls, ad[1], ad[0], sum(1 << e for e in es))
        count["ls"] += len(es)

    dma("a", "l_req", b("reqi"), hbm(T.req))
    LW = 2048 // LOADS
    for h in range(LOADS):
        dma("s", "l_rec%d" % h, b("reci", LW * h, LW * h + LW), (T.rec[:, LW * h:LW * h + LW], None, 0, 0))
    dma("s", "l_aim", b("aimb"), hbm(T.aim))
    dma("s", "l_wt", b("wtb"), hbm(T.wt))
    dma("s", "l_mul", b("muli"), hbm(T.mul))
    dma("s", "l_th", b("thi"), hbm(T.th))

    fill(b("ones"), 1.0)
    fill((T.offc[64:128, :], "offc", 0, 256), -1.0 / 256)
    o128 = b("ones", 0, 128)
    iota(b("p8"), [[0, 16]], 0, 1)
    iota(b("pb"), [[16, 16]], 0, 0)
    affine(b("idb"), o128, [[-1, 128]], A.is_equal, 0, 1)
    iota(b("colr"), [[0, 8], [1, 16]], 0, 0)
    affine(b("en", 0, 1024), b("ones", 0, 1024), [[-1, 64], [0, 16]], A.is_equal, 0, 1)
    affine(b("en", 1024, 2048), b("ones", 0, 1024), [[-1, 64], [0, 16]], A.is_equal, -64, 1)
    iota(b("xoff"), [[0, WID // 256], [256, 16], [0, 16]], -2048, 0)
    iota((T.offc[0:64, :], "offc", 0, 256), [[0, 16], [-4, 16]], 32, 0)
    iota(b("irow"), [[1, 256]], 0, 0)
    affine(b("bt"), o128, [[-16, 8], [0, 16]], A.is_ge, 0, 1)
    affine(b("bo"), b("bt"), [[16, 8], [0, 16]], A.is_ge, 15, -1)

    def selectors():
        for r in range(16):
            affine(sel(r), b("bo"), [[0, 8], [1, 16]], A.is_equal, -r, 0)
    fill(b("rm"), 1.0)
    fill(b("rm", 0, WID, 16), 0.0)
    fill(b("mhalf"), -0.5)
    fill(b("tiny"), 1.0 / 65536)
    tsc(b("pa"), b("p8"), 15, A.bitwise_and)
    tt(b("pc"), b("pa"), b("pb"), A.add)
    tsc(b("ic"), b("pc"), 1.0 / 512, A.mult)
    tsc(b("ic8"), b("pc"), 8.0, A.mult)
    copy(b("rcol"), b("pa", 0, 1))
    tsc(b("ocol"), b("pa", 0, 1), -2.0, A.mult, -1.0, A.add)
    tsc(b("ocol2"), b("pa", 0, 1), 2560.0, A.mult, 1280.0, A.add)
    for x, lo, hi in tokens(SCHED):
        if x == "K":
            act(b("kz", 16 * lo, 16 * hi), b("ones", 0, 16 * (hi - lo)), F.Copy, scale=0.0)
    act(b("nidb"), b("idb"), F.Copy, scale=-1.0)
    act(b("idh"), b("idb"), F.Copy)
    act(b("nb"), b("rm"), F.Identity, scale=-BIG, bias=BIG)

    def split(src="s2"):
        tsc(b("ki"), b(src), 7, A.bitwise_and)
        tsc(b("ni"), b(src), 3, A.arith_shift_right, 255, A.bitwise_and)

    def keyed(plain=False):
        act(b("nk"), b("ki"), F.Identity, scale=-512.0 if plain else 512.0, bias=1536.0 if plain else -2048.0)
        act(b("nib"), b("ni"), F.Identity, scale=-1.0 if plain else 1.0, bias=255.0 if plain else 0.0)
        mms(b("psN", 0, 256), [(b("nidb"), b("nk")), (b("nidb"), b("nib"))])

    def listed():
        act(b("cl"), b("psN", 0, 256), F.Identity, bias=1791.0)

    def kspread(lo, hi, first=False):
        if first or ("+", lo, hi) not in tokens(SCHED):
            copy(b("kz", 16 * lo, 16 * hi, 16), b("nk", lo, hi))
        scan(b("kb", 16 * lo, 16 * hi), b("rm", 0, 16 * (hi - lo)), b("kz", 16 * lo, 16 * hi), A.mult, A.add)

    turned = {"kt": [], "vt": []}

    def rows(name, n, lo, hi): return (T[name][0:n, lo:hi], name, lo, hi)

    def trans(dst, src, lo, hi, scale):
        if (lo, hi) not in turned[dst]:
            turned[dst].append((lo, hi))
        k = 128 * turned[dst].index((lo, hi))
        p = rows("psV", hi - lo, 256 + k % 256, 384 + k % 256)
        mms(p, [(b(src, lo, hi), b("idb"))])
        act(rows(dst, hi - lo, k, k + 128), p, F.Copy, scale=scale)

    def keys_t(h): trans("kt", "nk", 128 * h, 128 * h + 128, 1.0)
    def ring(lo, hi): return b("psS", 16 * lo % 2048, 16 * lo % 2048 + 16 * (hi - lo))

    def pspread(lo, hi, tname, now):
        h, (l, e) = [(j, x) for j, x in enumerate(turned[tname]) if x in now and x[0] <= lo and hi <= x[1]][0]
        k = 16 * (lo - l)
        mms(bank(lo, hi), [(rows(tname, e - l, 128 * h, 128 * h + 128), rows("en", e - l, k, k + 16 * (hi - lo)))], stop=False)

    def padd(lo, hi, data, ident):
        mms(bank(lo, hi), [(b(ident), b(data, 16 * lo, 16 * hi))], start=False)

    def bank(lo, hi):
        p = ring(lo, hi)
        return (p[0], p[1], p[2] // 512 * 512, p[2] // 512 * 512 + 512)

    def low(h): tsc(b("ra", LW * h, LW * h + LW), b("reci", LW * h, LW * h + LW), 2047, A.bitwise_and)
    def wide(h): act(b("rb", LW * h, LW * h + LW), b("ra", LW * h, LW * h + LW), F.Identity, scale=512.125, bias=-0.4375)

    def high(h):
        act(b("xt", LW * h, LW * h + LW), b("reci", LW * h, LW * h + LW), F.Identity, bias=1279.5 + 1.0 / 4096, scale=1.0 / 2048)

    def names(lo, hi):
        for k in range(8):
            tsc(b("dw", 512 * k + lo // 8, 512 * k + hi // 8), b("rb", lo + k, hi, 8), 3839, A.bitwise_and)
    split("reqi")
    keyed(True)
    low(0), wide(0), listed()
    tsc(b("offd"), b("colr"), b("rcol"), A.not_equal, 2 * BIG, A.mult)
    low(1), wide(1), keys_t(0), keys_t(1), high(0)
    for x, lo, hi in tokens(SCHED):
        if x == "K":
            kspread(lo, hi, True)
    low(2), wide(2), high(1), names(0, 2 * LW), low(3), wide(3), high(2)
    names(2 * LW, 4 * LW)

    def soon():
        high(3)
        act(b("hid"), b("idb"), F.Copy, scale=0.5)

    def late():
        for k in range(8):
            tsc(b("xw", 512 * k, 512 * k + 256), b("xt", k, 2048, 8), -1280.0, A.add)

    def later():
        act(b("aimc"), b("aimb"), F.Identity, scale=-1.0, bias=-1280.0)
        act(b("mid"), b("ones", 0, 256), F.Copy, scale=-1408.0)

    def latest():
        act(b("cw"), b("wtb"), F.Identity, scale=128.0, bias=-128.0)
        act(b("big"), b("idb"), F.Copy, scale=-4096.0)
        act(b("kcol"), b("muli"), F.Identity, scale=-1.0, bias=1920.0)
        act(b("tcol"), b("thi"), F.Copy)
        act(b("dk"), b("idb"), F.Copy, scale=b("kcol"))
        act(b("odd"), b("idb"), F.Copy, scale=b("ocol"))
        act(b("odd2"), b("idb"), F.Copy, scale=b("ocol2"))

    def zeros():
        spread = [k for k in tokens(SCHED + " " + SCHEDL) if k[0] == "j"]
        lo, hi = min(k[1] for k in spread), max(k[2] for k in spread)
        iota(b("vz", 16 * lo, 16 * hi), [[0, 16 * (hi - lo)]], 0, 0)

    def now(last): return tokens(SCHEDL if last else SCHED)

    DW, XW = b("dw"), b("xw")
    for t in range(STEPS):
        last = t == STEPS - 1
        CP, VV, PL, ACP, AV, APL = "cp%d" % t, "vv%d" % t, "pl%d" % t, "acp%d" % t, "av%d" % t, "apl%d" % t
        folded, toks = set(), set(now(last))

        def names_v(lo, hi):
            gtt(b("xb", 16 * lo, 16 * hi), DW, b("cl", lo, hi), b("kb", 16 * lo, 16 * hi), A.add)

        def names_abs(lo, hi):
            act(b("yb", 16 * lo, 16 * hi), b("xb", 16 * lo, 16 * hi), F.Abs, bias=-1791.0)

        def names_a(lo, hi):
            gact(b("xh", 16 * lo, 16 * hi), DW, b("cl", lo, hi), F.Identity, bias=-2048.0)

        def names_ps(lo, hi):
            act(b("yb", 16 * lo, 16 * hi), ring(lo, hi), F.Abs, bias=257.0)

        def least(lo, hi):
            scan(b("sc", 16 * lo, 16 * hi), b("nb", 0, 16 * (hi - lo)), b("yb", 16 * lo, 16 * hi), A.max, A.min)
            if ("Q", lo, hi) in toks:
                return mms(b("psN", 256 + lo, 256 + hi), [(b("idb"), b("nib", lo, hi)), (b("nidb"), b("sc", 16 * lo + 15, 16 * hi, 16))])
            tt(b("mm", lo, hi), b("sc", 16 * lo + 15, 16 * hi, 16), b("nib", lo, hi), A.min)
            o = b("psP", 256 + lo, 256 + hi) if ("R", lo, hi) in toks else b("psN", lo, hi)
            mms(o, [(b("nidb"), b("nk", lo, hi)), (b("nidb"), b("mm", lo, hi))])

        def raised(lo, hi):
            tsc(b(CP, lo, hi), b("psP", 256 + lo, 256 + hi), 1791.0, A.add)

        def rise(lo, hi):
            act(b("mm", lo, hi), b("psN", 256 + lo, 256 + hi), F.Relu)
            mms(b("psN", lo, hi), [(b("nidb"), b("nk", lo, hi)), (b("nidb"), b("nib", lo, hi)), (b("idb"), b("mm", lo, hi))])

        def risen(lo, hi):
            act(b(CP, lo, hi), b("psN", lo, hi), F.Identity, bias=1791.0)

        def values_v(lo, hi):
            gtt(b("xg", 16 * lo, 16 * hi), XW, b(CP, lo, hi), b("xoff", 0, 16 * (hi - lo)), A.add)

        def extremes_v(lo, hi):
            for m in range(16 * lo, 16 * hi, 256):
                scan(b("mx", m // 2, m // 2 + 128), b("xg", m, m + 256, 2), b("xg", m + 1, m + 256, 2), A.max, A.max, -4096.0)
            for m in range(16 * lo, 16 * hi, 256):
                scan(back("mn", m // 2, m // 2 + 128), back("xg", m, m + 256, 2), back("xg", m, m + 255, 2), A.min, A.min, 4096.0)
            mms(b("psE", lo, hi), [(o128, b("offc", lo, hi)), (b("hid"), b("mx", 8 * lo + 7, 8 * hi, 8)),
                                   (b("hid"), b("mn", 8 * lo, 8 * hi, 8))])

        def values_a(lo, hi):
            gact(b("xg", 16 * lo, 16 * hi), XW, b(CP, lo, hi), F.Copy)

        def extremes_a(lo, hi):
            w, e = (16 * lo, 16 * hi), (16 * lo + 15, 16 * hi, 16)
            scan(b("mxa", *w), b("rm", 0, 16 * (hi - lo)), b("xg", *w), A.mult, A.max)
            scan(b("mna", *w), b("nb", 0, 16 * (hi - lo)), b("xg", *w), A.max, A.min)
            if ("#", lo, hi) not in toks:
                mms(b("psE", lo, hi), [(b("hid"), b("mhalf", 0, hi - lo)), (b("hid"), b("mxa", *e)), (b("hid"), b("mna", *e))])

        def halved_v(lo, hi):
            e = (16 * lo + 15, 16 * hi, 16)
            tt(b("zs", lo, hi), b("mxa", *e), b("mna", *e), A.add)
            tsc(b("zb", lo, hi), b("zs", lo, hi), 0.5, A.mult, 1279.75, A.add)

        def halved(lo, hi, scalar):
            if scalar:
                act(b("zb", lo, hi), b("psE", lo, hi), F.Identity, bias=1280.0)
            else:
                tsc(b("zb", lo, hi), b("psE", lo, hi), 1280.0, A.add)

        def less_mid(lo, hi):
            mms(b("psP", 256 + lo, 256 + hi), [(b("idb"), b("mid", lo, hi)), (b("idh"), b("zb", lo, hi))])

        def less_aim(lo, hi):
            mms(b("psV", lo, hi), [(b("idh"), b("aimc", lo, hi)), (b("idh"), b("zb", lo, hi))])

        def weigh(lo, hi):
            tt(b("zw", lo, hi), b("psP", 256 + lo, 256 + hi), b("wtb", lo, hi), A.mult)

        def weigh_v(lo, hi):
            tsc(b("zc", lo, hi), b("zb", lo, hi), -1408.0, A.add)
            tt(b("zw", lo, hi), b("zc", lo, hi), b("wtb", lo, hi), A.mult)

        def places_sum(lo, hi):
            q0, q1 = lo // 16, hi // 16
            mms(b("psP", q0, q1), [(b("idb"), b("ic", q0, q1))] + [(sel(r), b("zw", lo + r, hi, 16)) for r in range(16)])

        def places_wide(lo, hi):
            mms(b("psP", 256 + lo, 256 + hi), [(b("tiny"), b("irow", lo, hi)), (b("idb"), b("offd", 0, hi - lo)), (b("bo"), b("zw", lo, hi))])

        def places(lo, hi):
            q0, q1 = lo // 16, hi // 16
            if ("f", lo, hi) in toks:
                scan(b("ud", lo, hi), b("nb", 0, hi - lo), b("psP", 256 + lo, 256 + hi), A.add, A.min)
                tsc(b("pi", q0, q1), b("ud", lo + 15, hi, 16), 512.0, A.mult)
            else:
                tsc(b("pi", q0, q1), b("psP", q0, q1), 512.0, A.mult)
            tsc(b("p9" if last else PL, q0, q1), b("pi", q0, q1), 3839, A.bitwise_and)
            copy(b("plu", q0, q1), b("p9" if last else PL, q0, q1))

        def pick(lo, hi): scan(b("ud", lo, hi), b("nb", 0, hi - lo), b("psP", 256 + lo, 256 + hi), A.add, A.min)

        def place_a(lo, hi):
            src = b("ud", lo + 15, hi, 16) if ("f", lo, hi) in toks else b("psP", lo // 16, hi // 16)
            act(b("pi", lo // 16, hi // 16), src, F.Identity, scale=512.0)

        def place_b(lo, hi): tsc(b("p9" if last else PL, lo // 16, hi // 16), b("pi", lo // 16, hi // 16), 3839, A.bitwise_and)
        def place_c(lo, hi): act(b("plu", lo // 16, hi // 16), b("p9" if last else PL, lo // 16, hi // 16), F.Copy)

        def send_places():
            if last:
                tsc(b("pi"), b("p9"), 9, A.logical_shift_right)
                tt(b(PL), b("pi"), b("ic8"), A.add)
            send(t, APL, PL, "rp%d" % t, 0, 16)

        def spread_v(lo, hi):
            if not [k for k in toks if k[0] == "t" and k[1] <= lo and hi <= k[2]]:
                copy(b("vz", 16 * lo, 16 * hi, 16), b(AV, lo, hi))
            scan(b("vb", 16 * lo, 16 * hi), b("rm", 0, 16 * (hi - lo)), b("vz", 16 * lo, 16 * hi), A.mult, A.add)

        def judge_v(lo, hi):
            for m in range(lo, hi, 16):
                gtt((T.dg[:, m // 16, :], "dg", 16 * m, 16 * m + 256), XW, b(ACP, m, m + 16), b("vb", 16 * m, 16 * m + 256), A.subtract)

        def judge_fold(lo, hi):
            tsc(four("ab", lo, hi), four("dg", lo, hi), 0.0, A.min, -2.0, A.mult)
            folded.add(lo)

        def judge_a(lo, hi):
            gact(b("gx", 16 * lo, 16 * hi), XW, b(ACP, lo, hi), F.Copy)

        def esum(lo, hi):
            src = ["ab", "dg"] if lo in folded else ["ab"]
            mms(b("psE", 256 + lo, 256 + hi), [(sel(r), four(x, lo, hi, r)) for x in src for r in range(16)])

        def verdict(lo, hi):
            q0, q1 = lo // 16, hi // 16
            tsc(b("okm", lo, hi), b("psE", 256 + lo, 256 + hi), b("tcol"), A.is_lt)
            scan(b("cnt", lo, hi), b("rm", 0, hi - lo), b("okm", lo, hi), A.mult, A.add)
            tsc(b("t1", q0, q1), b("cnt", lo + 15, hi, 16), 6.5, A.is_lt, 2048.0 if last else 256.0, A.mult)
            tt(b("t2", q0, q1), b("t1", q0, q1), b(APL, q0, q1), A.add)
            if ("*", lo, hi) not in toks:
                tsc(b("off", q0, q1), b("t2", q0, q1), -8.0 * lo if last else 0.0, A.add)

        def offsets(lo, hi):
            act(b("off", lo // 16, hi // 16), b("t2", lo // 16, hi // 16), F.Identity, bias=-8.0 * lo if last else 0.0)

        def usum():
            mms(b("psE", 0, 256), [(b("bo"), b("cw")), (b("bo"), b("zw"))])

        def ucut():
            act(b("hq"), b("psE", 0, 256), F.Identity, scale=1.0 / 4096, bias=192.0)
            mms(b("psN", 0, 256), [(b("bo"), b("cw")), (b("bo"), b("zw")), (b("big"), b("hq"))])

        def square():
            act(b("uc"), b("psN", 0, 256), F.Identity, bias=192.0 * 4096)
            mms(b("psP", 256, 512), [(b("odd2"), b("ones", 0, 256)), (b("odd"), b("zb")), (b("dk"), b("uc"))])
            act(b("sq"), b("psN", 0, 256), F.Square, bias=192.0 * 4096)
            act(b("sh"), b("sq"), F.Identity, scale=-1.0 / 32, bias=-16.5 / 32)

        def nextreq():
            tt(b("s2"), b("sh"), b("psP", 256, 512), A.add)
            if last:
                tsc(b("cr"), b("s2"), 2047, A.bitwise_and)

        def small_out():
            act(b("yco"), b("cr"), F.Identity, scale=-1.0, bias=2047.0)
            dma("s", "o_yc", hbm(T.yc), b("yco"))

        def z_out():
            act(b("zo"), b("zb"), F.Identity, bias=-1280.0)
            dma("s", "o_yz", hbm(T.yz), b("zo"))

        def arrive_x():
            if t == 0:
                late()
            else:
                put(XW, b("off"), b("av%d" % (t - 1)))

        def yo_own():
            for k in range(8):
                if k < YG:
                    affine(b("yo", k, 2048, 8), b("xw", 512 * k, 512 * k + 256), [[0, 256]], A.is_ge, 0, 0)
                else:
                    copy(b("yo", k, 2048, 8), b("xw", 512 * k, 512 * k + 256))

        def final(lo, hi):
            put(b("yo", 8 * lo, 8 * hi + 2048), b("off", lo // 16, hi // 16), b(AV, lo, hi))
            dma("s", "o_yx%d" % lo, (T.yx[:, 8 * lo:8 * hi], None, 0, 0), b("yo", 8 * lo, 8 * hi))

        RANGED = {"n": names_v, "b": names_abs, "A": names_a, "B": names_ps, "r": least, "R": raised, "g": values_v, "h": extremes_v,
                  "G": values_a, "H": extremes_a, "O": risen, "Q": rise, "<": pick, "#": halved_v, "*": offsets,
                  "t": lambda lo, hi: act(b("vz", 16 * lo, 16 * hi, 16), b(AV, lo, hi), F.Copy),
                  "+": lambda lo, hi: act(b("kz", 16 * lo, 16 * hi, 16), b("nk", lo, hi), F.Copy), "5": place_a, "6": place_b, "7": place_c, "z": weigh, "Z": weigh_v, "3": less_mid, "4": less_aim, "f": places_wide,
                  "i": lambda lo, hi: halved(lo, hi, False), "I": lambda lo, hi: halved(lo, hi, True), "p": places_sum, "q": places, "j": spread_v, "w": judge_v,
                  "m": judge_fold, "J": judge_a, "e": esum, "v": verdict, "E": final, "K": kspread,
                  "8": lambda lo, hi: pspread(lo, hi, "kt", [(0, 128), (128, 256)]), "1": lambda lo, hi: padd(lo, hi, "xh", "idh"),
                  "T": lambda lo, hi: trans("vt", AV, lo, hi, -1.0),
                  "9": lambda lo, hi: pspread(lo, hi, "vt", [k[1:] for k in tokens(SCHEDL if last else SCHED) if k[0] == "T"]),
                  "2": lambda lo, hi: padd(lo, hi, "gx", "idb"),
                  "a": lambda lo, hi: act(b(VV, lo, hi), b("psV", lo, hi), F.Abs),
                  "k": lambda lo, hi: act(four("ab", lo, hi), ring(lo, hi), F.Abs),
                  "o": lambda lo, hi: act(four("ab", lo, hi), four("dg", lo, hi), F.Abs),
                  "c": lambda lo, hi: send(t, ACP, CP, "rc%d_%d" % (t, lo), lo, hi),
                  "s": lambda lo, hi: send(t, AV, VV, "rs%d_%d" % (t, lo), lo, hi),
                  "x": lambda lo, hi: put(XW, b("plu", lo // 16, hi // 16), b(VV, lo, hi)),
                  "d": lambda lo, hi: put(DW, b("plu", lo // 16, hi // 16), b(CP, lo, hi)),
                  "D": lambda lo, hi: put(DW, b("off", lo // 16, hi // 16), b(ACP, lo, hi))}
        ONCE = {"X": arrive_x, "u": usum, "y": ucut, "S": square, "N": nextreq, "L": split, "l": keyed, "M": listed,
                "Y": yo_own, "P": send_places, "C": small_out, "F": z_out, "W": later if t == 0 else lambda: None,
                "0": soon if t == 0 else lambda: None, "/": selectors if t == 0 else lambda: None,
                "%": zeros if t == 0 else lambda: None, "V": latest if t == 0 else lambda: None}
        for k, lo, hi in tokens(SCHEDL if last else SCHED):
            if k in RANGED:
                RANGED[k](lo, hi)
            elif k == "U":
                keys_t(lo)
            else:
                ONCE[k]()
    for s in sorted(count):
        g.wait_ge(T.sem[s], count[s])
